import numpy as np, ml_dtypes
CORES = [23,119,17,113]
N = 4
BF = ml_dtypes.bfloat16
W, R, P, STEPS, HOPS, SHIFT = 2048, 4096, 256, 4, 4, 1
def parts(rng):
    h = rng.integers(0, 256, (N, 8, 16, P)); w = rng.integers(0, 256, (N, 8, 16, 1)); t = rng.integers(700, 1300, (N, 8, 16, 1))
    m = rng.random((N, 8, W)) < rng.choice(np.array([0.1, 0.25, 0.5]), (N, 8, 1))
    return h, w, t, m, rng.integers(0, R, (N, 8, 16, W)), rng.integers(0, 256, (N, 8, 16, R))
def pack(h, w, t, m, o, r):
    m = m.astype(np.int32); m[..., 0] = 1
    b = lambda v, n: np.ascontiguousarray(v.reshape(N, 128, n)).astype(np.float32).astype(BF)
    i = lambda v, n: np.ascontiguousarray(v.reshape(N, 128, n)).astype(np.int32)
    return {"h0": b(h, P), "w": b(w, 1), "th": i(t, 1), "marks": m, "owner": i(o, W), "hdr": b(r, R)}
def far(rng, h, t, o, r, g, u=None):
    r[:, g] = rng.integers(128, 192, (N, 16, R))
    goal = np.where(np.arange(R) % 2 == 0, 4, 0) + rng.integers(0, 4, (N, R))
    r[:, g, 15] = 128 + ((goal - np.sum(r[:, g, :15], axis=1)) & 63)
    o[:, g] = (o[:, g] & -2) + (np.arange(16) & 1)[:, None]
    h[:, g] = rng.integers(0, 16, (N, 16, P))
    if u is not None: h[:, g, 0] = u >> 4; h[:, g, 1] = u & 15
    h[:, g, 15] = (-np.sum(h[:, g, :15], axis=1)) & 63
    t[:, g] = rng.integers(1300, 1751, (N, 16, 1))
def setup_inputs(rng):
    return pack(*parts(rng))
def setup_inputs_crowd(rng):
    h, w, t, m, o, r = parts(rng)
    w[:, 0::4] = 0; t[:, 0::4] = rng.integers(500, 1100, (N, 2, 16, 1))
    w[:, 1::4] = 0; w[:, 1::4, 0] = rng.integers(1, 4, (N, 2, 1)); h[:, 1::4, 0] = rng.integers(0, 3, (N, 2, P))
    w[:, 2::4] = 128 * rng.integers(0, 2, (N, 2, 16, 1))
    n = P // 16; lane = np.arange(P)
    far(rng, h, t, o, r, 4)
    start = rng.integers(0, n, (N, 16)); start[:, 0::4] = 0; start[:, 1::4] = n - 1; start[:, 3::4] = 1
    near = (lane >> 4) < start[:, lane & 15]
    h[:, 4] = np.where(near[:, None, :], rng.integers(128, 192, (N, 16, P)), h[:, 4])
    k = np.arange(256); found = np.unique((((k * k) >> 5) + k) & (W - 16), return_index=True)[1]
    order = np.argsort(rng.random((N, 16, len(found))), axis=-1)[..., :n]
    far(rng, h, t, o, r, 7, found[order].transpose(0, 2, 1).reshape(N, P))
    w[:, 7] = 0; w[:, 7, 0] = 16; w[:, 7, 1] = 1; m[:, 7] = True
    return pack(h, w, t, m, o, r)
def setup_inputs_ends(rng):
    h, w, t, m, o, r = parts(rng)
    k = np.arange(4096); tops = np.flatnonzero(((((k * k) >> 5) + k) & (W - 16)) == W - 16)
    u = rng.integers(0, 4096, (N, 6, P)); u[..., 0::32] = 0; u[..., 15::32] = rng.choice(tops, u[..., 15::32].shape)
    u[:, 4, 5::8] = rng.choice(tops, u[:, 4, 5::8].shape)
    w[:, :6] = 0; w[:, :6, 0] = 16; w[:, :6, 1] = 1; h[:, :6, 0] = u >> 4; h[:, :6, 1] = u & 15
    m[:, 0] = False; m[:, 1] = True; m[:, 2] = False; m[:, 2, W - 1] = True; m[:, 3] = True; m[:, 3, W - 1] = False; m[:, 4] = False; m[:, 4, 1] = True; m[:, 4, W - 16] = True
    t[:, 0:4:2] = rng.integers(0, 900, (N, 2, 16, 1)); t[:, 1] = rng.choice(np.array([0, 4096]), (N, 16, 1)); t[:, 5] = 0; t[:, 6] = 4096
    w[:, 7] = 255 - rng.integers(0, 16, (N, 16, 1)); h[:, 7] = 255 - rng.integers(0, 24, (N, 16, P)); w[0, 7] = 255; h[0, 7, :, 0::32] = 255
    return pack(h, w, t, m, o, r)
def setup_inputs_ties(rng):
    h, w, t, m, o, r = parts(rng)
    unit = rng.choice(np.array([8, 16]), (N, 8, 1, 1)); h = unit * (h // unit); r = unit * (r // unit)
    t = unit * (t // unit) + rng.choice(np.array([0, 0, 0, 1, -1]), t.shape)
    w[:, :2] = 0; m[:, :2, :16] = True; h[:, 1, :, :16] = 0; h[:, 1, 0, 1:16:2] = 1
    i = np.arange(16)
    for q in range(N):
        t[q, 0, :, 0] = np.sum(np.abs(r[q, 0][:, o[q, 0, :, 0]] - h[q, 0, :, 0:1]), axis=0)
        t[q, 1, :, 0] = np.sum(np.abs(r[q, 1][:, o[q, 1, i, i]] - h[q, 1, :, :16]), axis=0) + (i % 2 == 0)
    return pack(h, w, t, m, o, r)
def setup_inputs_alike(rng):
    h, w, t, m, o, r = parts(rng)
    o[:, ::2] = rng.choice(np.array([0, R - 1, R // 2, 3]), (N, 4, 16, W)); o[:, 1::4] = o[:, 1::4, :1].copy()
    r[..., 0] = 0; r[..., R - 1] = 255
    h[..., 0::7] = 0; h[..., 1::7] = 255; h[..., 3::7] = r[..., R // 2][..., None]
    t[:, 2] = 1
    t[:, 4] = 4080; t[:, 4, 1::4] = rng.choice(np.array([4081, 4096]), (N, 4, 1)); o[:, 4, 1::4] = R - 1; o[:, 4, 12] = 3
    t[:, 6] = 0; o[:, 6, 1::4] = R // 2; o[:, 6, 0] = 3
    return pack(h, w, t, m, o, r)
def setup_inputs_spread(rng):
    h, w, t, m, o, r = parts(rng)
    h = (np.exp2(8 * rng.random((N, 8, 1, P))) * rng.random((N, 8, 16, P))).astype(np.int64)
    r = (np.exp2(8 * rng.random((N, 8, 1, R))) * rng.random((N, 8, 16, R))).astype(np.int64)
    w = np.minimum(np.exp2(8 * rng.random((N, 8, 16, 1))).astype(np.int64), 255)
    t = np.minimum(np.exp2(12 * rng.random((N, 8, 16, 1))).astype(np.int64), 4096)
    m = rng.random((N, 8, W)) < np.exp2(-8 * rng.random((N, 8, 1)))
    o = np.minimum((R * rng.random((N, 8, 16, W)) ** 3).astype(np.int64), R - 1)
    return pack(h, w, t, m, o, r)
def check_inputs(d):
    bad = []
    for k, hi in (("h0", 255), ("w", 255), ("th", 4096), ("marks", 1), ("owner", R - 1), ("hdr", 255)):
        v = np.asarray(d[k]).astype(np.float32)
        if not np.all((v >= 0) & (v <= hi) & (v == np.floor(v))): bad.append("range of " + k)
    if not np.all(np.asarray(d["marks"])[..., 0] == 1): bad.append("address 0 is a boundary")
    return bad
def reference(h0, w, th, marks, owner, hdr):
    h = h0.astype(np.float32).astype(np.int64).reshape(N, 8, 16, P); wt = w.astype(np.float32).astype(np.int64).reshape(N, 8, 16, 1)
    t = th.astype(np.int64).reshape(N, 8, 1, 16); m = marks > 0; o = owner.astype(np.int64).reshape(N, 8, 16, W)
    r = hdr.astype(np.float32).astype(np.int32).reshape(N, 8, 16, R)
    port = np.arange(P) & 15; slot = np.arange(16)
    for step in range(STEPS):
        u = np.add.reduce(wt * h, axis=2) & 4095
        x = ((((u * u) >> 5) + u) & (W - 16)) + port
        top = np.maximum.accumulate(np.where(m, np.arange(W), 0), axis=2)
        a = np.take_along_axis(top, x, 2); b = np.take_along_axis(top, (a - 1) & (W - 1), 2)
        ra = np.take_along_axis(o, a[:, :, None, :], 3); rb = np.take_along_axis(o, b[:, :, None, :], 3)
        new = []
        for q in range(N):
            ids = np.ascontiguousarray(ra[q].transpose(0, 2, 1)).reshape(8, 1, P * 16)
            v = np.take_along_axis(r[q], ids, 2).reshape(8, 16, P, 16)
            d = np.add.reduce(np.abs(v - h[q][..., None]), axis=1)
            n = np.where(d < t[q], slot, (d >> 2) & 15)
            e = np.zeros((8, P), np.int64) + port
            for hop in range(HOPS):
                e = np.take_along_axis(n, e[..., None], 2)[..., 0]
            done = np.take_along_axis(n, e[..., None], 2)[..., 0] == e
            ve = np.take_along_axis(v, e[:, None, :, None], 3)[..., 0]
            new.append(np.where(done[:, None, :], (h[q] + ve) >> 1, np.abs(h[q] - ve)))
            col = np.where(slot[None, :, None] == e[:, None, :], rb[q], ra[q])
            for g in range(8):
                lanes = np.flatnonzero(~done[g])
                xs, first = np.unique(x[q, g, lanes], return_index=True)
                o[q, g][:, xs] = col[g][:, lanes[first]]
                m[q, g, xs] = True
        h = np.roll(np.stack(new), SHIFT, axis=0)
    return {"yh": h.reshape(N, 128, P).astype(np.float32).astype(BF), "yo": o.reshape(N, 128, W).astype(np.float32), "ym": m.astype(np.float32)}

@@ -1,0 +1,495 @@
+from concourse.mybir import AluOpType as A, ActivationFunctionType as F
+
+N, STEPS, W, R, P = 4, 4, 2048, 4096, 256
+PIECES = [(8, 16), (0, 8)]
+NPC = len(PIECES)
+VCH = [(0, 32), (32, 64)]
+ACH = [(64, 96), (96, 128)]
+NCH = [(0, 64), (64, 128)]
+VL = 64
+TW = W + P
+HEXP = "agavaagavaagavag"
+
+SCRATCH = {
+    "HD": ("sbuf", [128, R], "bfloat16"), "OW": ("sbuf", [128, W], "int32"), "MK": ("sbuf", [128, 128], "int32"),
+    "MB": ("sbuf", [128, 128], "bfloat16"), "WT": ("sbuf", [128, 1], "bfloat16"), "TI": ("sbuf", [128, 1], "int32"),
+    "YO": ("sbuf", [128, TW], "float32"), "MZ": ("sbuf", [128, TW], "float32"), "NM": ("sbuf", [128, TW], "float32"),
+    "ZP": ("sbuf", [128, W + 8], "float32"), "YM": ("sbuf", [128, W], "float32"),
+    "PI": ("sbuf", [128, 1], "int32"), "SI": ("sbuf", [128, 1], "int32"), "SJ": ("sbuf", [128, 1], "int32"),
+    "SC": ("sbuf", [128, 1], "float32"), "SQ": ("sbuf", [128, 1], "float32"), "TH": ("sbuf", [128, 1], "float32"),
+    "BIG": ("sbuf", [128, 1], "float32"), "SB": ("sbuf", [128, 1], "float32"),
+    "ON": ("sbuf", [128, 128], "bfloat16"), "B1": ("sbuf", [128, 128], "bfloat16"), "BO": ("sbuf", [128, 128], "bfloat16"),
+    "HB": ("sbuf", [128, 128], "bfloat16"), "ID": ("sbuf", [128, 128], "bfloat16"), "IH": ("sbuf", [128, 128], "bfloat16"),
+    "NI": ("sbuf", [128, 128], "bfloat16"),
+    "S1": ("sbuf", [128, 128], "bfloat16"), "S2": ("sbuf", [128, 128], "bfloat16"), "DB": ("sbuf", [128, 128], "bfloat16"),
+    "IK": ("sbuf", [128, 16], "float32"), "OH": ("sbuf", [128, 16], "float32"),
+    "CM": ("sbuf", [128, 2048], "bfloat16"), "SR": ("sbuf", [128, 2048], "bfloat16"), "BW": ("sbuf", [128, 128], "bfloat16"),
+    "WU": ("sbuf", [128, 512], "bfloat16"), "HL": ("sbuf", [128, 512], "bfloat16"), "DG": ("sbuf", [128, 512], "float32"),
+    "IQ": ("sbuf", [128, 64], "float32"), "MQ": ("sbuf", [128, 64], "float32"), "RS": ("sbuf", [128, 64], "float32"),
+    "JS": ("sbuf", [128, 128], "float32"), "G1": ("sbuf", [128, 128], "float32"), "G0": ("sbuf", [128, 128], "bfloat16"),
+    "T0": ("sbuf", [128, 16], "float32"), "TR": ("sbuf", [128, 16], "float32"),
+    "BR": ("sbuf", [1, 128], "bfloat16"), "OB": ("sbuf", [1, 128], "bfloat16"), "CR": ("sbuf", [1, 64], "bfloat16"),
+    "ZE": ("sbuf", [128, 64], "float32"),
+    "LP": ("sbuf", [128, P], "uint16"), "ZA": ("sbuf", [128, P], "float32"), "ZB": ("sbuf", [128, P], "float32"),
+    "DZ": ("sbuf", [128, P], "float32"), "HX": ("sbuf", [128, 16 * P], "bfloat16"), "hn": ("sbuf", [128, P * STEPS], "bfloat16"),
+}
+for _b in range(8):
+    SCRATCH["ps%d" % _b] = ("psum", [128, 512], "float32")
+for _t in range(STEPS + 1):
+    SCRATCH["hb%d" % _t] = ("sbuf", [128, P], "bfloat16")
+_WIDE = {
+    "D": (16, "bfloat16"), "AB": (16, "bfloat16"), "NA": (1, "float32"), "NX": (1, "int32"), "NN": (1, "int32"),
+    "NB": (1, "bfloat16"), "Y": (1, "bfloat16"), "SG": (1, "bfloat16"), "E4": (1, "bfloat16"), "DS": (1, "bfloat16"),
+    "FD": (1, "int32"), "TD": (1, "bfloat16"), "QD": (1, "bfloat16"), "DE": (1, "float32"), "CL": (1, "int32"),
+}
+_SMALL = {"EL": "uint16", "DW": "float32", "DT": "float32", "XQ": "float32", "DU": "float32", "T2": "float32",
+          "T3": "float32", "DM": "float32", "DX": "float32", "SL": "uint16"}
+_QUAD = ["EM", "ES", "FM", "FS"]
+PLACE = {}
+for _p, (_c0, _c1) in enumerate(PIECES):
+    _nc = _c1 - _c0
+    for _n, (_k, _d) in _WIDE.items():
+        SCRATCH["%s%d" % (_n, _p)] = ("sbuf", [128, _k * 16 * _nc], _d)
+        PLACE[_n, _p] = ("%s%d" % (_n, _p), 0, _k * 16 * _nc)
+_fill = {}
+for _p, _ns in [(k, list(_SMALL.items()) + [(n, "float32") for n in _QUAD]) for k in range(NPC)] + [(None, [
+        ("UM", "float32"), ("US", "float32"), ("ZM", "float32"), ("ZS", "float32"), ("UI", "int32"), ("UA", "int32"),
+        ("UB", "int32"), ("UP", "int32"), ("UX", "int32"), ("XF", "float32"), ("LX", "uint16"), ("OI", "int32"),
+        ("FR", "float32"), ("AL", "float32"), ("AM", "float32"), ("LA", "uint16")])]:
+    _nc = 16 if _p is None else PIECES[_p][1] - PIECES[_p][0]
+    for _n, _d in _ns:
+        _w = 4 * _nc if _n in _QUAD + ["UM", "US", "ZM", "ZS"] else _nc
+        PLACE[_n, _p] = ("sm_" + _d, _fill.get(_d, 0), _w)
+        _fill[_d] = _fill.get(_d, 0) + -(-_w // 16) * 16
+for _d, _w in _fill.items():
+    SCRATCH["sm_" + _d] = ("sbuf", [128, _w], _d)
+SEMAPHORES = ["qv", "qa", "qp", "qg", "ls"] + ["dm%d" % k for k in range(24)] + \
+    ["ar%d%d" % (t, p) for t in range(1, STEPS + 1) for p in range(NPC)]
+
+
+def rank_program(g, core, T, topo):
+    rank = T.rank_of(core)
+    if rank is None:
+        return
+    dst = T.cores[(rank + 1) % N]
+    rid, pid, _e = topo.addr(dst)
+    mask = topo.mask(core, dst)
+    ne = len(topo.engines(core, dst))
+    eng = {"v": g.vector, "a": g.scalar, "p": g.tensor, "g": g, "s": g.sync}
+    CY = 1.0e-3
+    ops = []
+
+    def r(n, lo=None, hi=None, st=1, p=None):
+        b, o, w = PLACE[n, p] if (n, p) in PLACE else (n, 0, SCRATCH[n][1][1])
+        return (b, o + (0 if lo is None else lo), o + (w if hi is None else hi), st)
+
+    def ap(x):
+        if not isinstance(x, tuple):
+            return x
+        b, lo, hi, st = x
+        if SCRATCH[b][1][0] == 1:
+            return T[b][0:1, lo:hi]
+        return T[b][:, lo:hi] if st == 1 else T[b][:, lo:hi:st]
+
+    def cnt(x):
+        return -(-(x[2] - x[1]) // x[3])
+
+    def ps(x):
+        return isinstance(x, tuple) and x[0][:2] == "ps"
+
+    def two(*xs):
+        return all(SCRATCH[x[0]][2] in ("bfloat16", "uint16") for x in xs)
+
+    def op(q, fn, rd, wr, dur, sem=None, lat=0.0):
+        ops.append({"q": q, "fn": fn, "rd": [x for x in rd if isinstance(x, tuple)], "wr": wr, "dur": dur,
+                    "sem": sem, "lat": lat})
+
+    def tt(o, a, b, f):
+        c = cnt(o) * (1 if ps(a) or ps(b) else 2)
+        op("v", lambda e: e.tensor_tensor(out=ap(o), in0=ap(a), in1=ap(b), op=f), [a, b], [o], max(64, c) * CY)
+
+    def ts(o, a, s1, f0, s2=None, f1=None):
+        c = cnt(o) * (0.5 if two(o, a) else 1)
+        if f1 is None:
+            fn = lambda e: e.tensor_scalar(out=ap(o), in0=ap(a), scalar1=ap(s1), scalar2=None, op0=f0)
+        else:
+            fn = lambda e: e.tensor_scalar(out=ap(o), in0=ap(a), scalar1=ap(s1), scalar2=ap(s2), op0=f0, op1=f1)
+        op("v", fn, [a, s1, s2], [o], max(64, c) * CY)
+
+    def cp(o, a):
+        c = cnt(o) * (0.5 if two(o, a) else 1)
+        op("v", lambda e: e.tensor_copy(out=ap(o), in_=ap(a)), [a], [o], max(64, c) * CY)
+
+    def scan(o, a, b, ini=0.0):
+        op("v", lambda e: e.tensor_tensor_scan(out=ap(o), data0=ap(a), data1=ap(b), initial=ap(ini), op0=A.mult, op1=A.add),
+           [a, b, ini], [o], max(64, cnt(o)) * CY)
+
+    def ms(o, k):
+        op("v", lambda e: e.memset(ap(o), k), [], [o], max(64, cnt(o) * (0.5 if two(o) else 1)) * CY)
+
+    def act(o, a, f, bias=0.0, scale=1.0):
+        op("a", lambda e: e.activation(out=ap(o), in_=ap(a), func=f, bias=ap(bias), scale=ap(scale)), [a, bias, scale], [o],
+           max(64, cnt(o)) * CY + 0.03)
+
+    def gat(q, o, w, off, in1=None, f=None):
+        d = 0.05 + 1.5 * cnt(o) * CY
+        if q == "a":
+            op("a", lambda e: e.activation(out=ap(o), in_=ap(w).indirect(ap(off)), func=F.Copy), [w, off], [o], d + 0.015)
+        elif in1 is None:
+            op("v", lambda e: e.tensor_copy(out=ap(o), in_=ap(w).indirect(ap(off))), [w, off], [o], d)
+        else:
+            op("v", lambda e: e.tensor_tensor(out=ap(o), in0=ap(w).indirect(ap(off)), in1=ap(in1), op=f), [w, off, in1], [o], d)
+
+    def mm(o, pairs, x4=1):
+        def fn(e):
+            last = None
+            for k, (l, x) in enumerate(pairs):
+                last = e.matmul(ap(o), ap(l), ap(x), k == 0, k == len(pairs) - 1)
+            return last
+        op("p", fn, [y for x in pairs for y in x], [o], len(pairs) * max(64, cnt(o)) * CY * x4)
+
+    ndma = [0]
+
+    def dma(q, o_fn, i_fn, rd, wr, dur):
+        s = "dm%d" % ndma[0]
+        ndma[0] += 1
+        op(q, lambda e: e.dma_start(out=o_fn(), in_=i_fn()), rd, wr, 0.1, sem=(s, 16), lat=dur)
+
+    def lanes(p):
+        return 16 * PIECES[p][0], 16 * PIECES[p][1]
+
+    dma("s", lambda: T.MK[:], lambda: T.marks[:], [], [r("MK")], 2.0)
+    dma("a", lambda: T.hb0[:], lambda: T.h0[:], [], [r("hb0")], 2.0)
+    for b in range(4):
+        lo, hi = 512 * b, 512 * b + 512
+        dma("s", lambda lo=lo, hi=hi: T.OW[:, lo:hi], lambda lo=lo, hi=hi: T.owner[:, lo:hi], [], [r("OW", lo, hi)], 2.5 + b)
+    dma("s", lambda: T.WT[:], lambda: T.w[:], [], [r("WT")], 2.0)
+    dma("s", lambda: T.HD[:], lambda: T.hdr[:], [], [r("HD")], 7.0)
+    dma("s", lambda: T.TI[:], lambda: T.th[:], [], [r("TI")], 3.0)
+
+    def iota(o, pat, base, cm):
+        op("g", lambda e: e.iota(ap(o), pat, base, cm, allow_small_or_imprecise_dtypes=True), [], [o],
+           0.13 + 2 * cnt(o) * CY)
+
+    def zero(o):
+        iota(o, [[0, cnt(o)]], 0, 0)
+
+    def sel(o, a, pat, f, base, cm):
+        op("g", lambda e: e.affine_select(out=ap(o), in_=ap(a), pattern=pat, compare_op=f, fill=0.0, base=base,
+                                          channel_multiplier=cm), [a], [o], 0.17 + 2 * cnt(o) * CY)
+    iota(r("PI"), [[0, 1]], 0, 1)
+    ms(r("ON"), 1.0)
+    ts(r("SI"), r("PI"), 15, A.bitwise_and)
+    cp(r("SC"), r("SI"))
+    sel(r("B1"), r("ON"), [[-16, 8], [0, 16]], A.is_ge, 0, 1)
+    sel(r("BO"), r("B1"), [[16, 8], [0, 16]], A.is_ge, 15, -1)
+    iota(r("IK"), [[1, 16]], 0, 0)
+    ts(r("OH"), r("IK"), r("SC"), A.is_equal)
+    for k in range(16):
+        act(r("SR", 128 * k, 128 * k + 128), r("BO"), F.Copy, 0.0, r("OH", k, k + 1))
+    cp(r("MB"), r("MK"))
+    ms(r("ZP", 0, 8), 0.0)
+    for b in range(4):
+        lo, hi = 512 * b, 512 * b + 512
+        for k in range(4 * b, 4 * b + 4):
+            mm(r("ps%d" % b, 128 * (k % 4), 128 * (k % 4) + 128), [(r("SR", 128 * k, 128 * k + 128), r("MB"))])
+        m, n2 = r("ps%d" % b), r("ps%d" % (4 + b))
+        act(n2, m, F.Copy, 1 / 4096, -1 / 4096)
+        act(r("NM", lo, hi), m, F.Copy, 1.0, -1.0)
+        tt(r("MZ", lo, hi), r("OW", lo, hi), m, A.mult)
+        tt(r("MZ", lo, hi), r("MZ", lo, hi), n2, A.add)
+        scan(r("ZP", 8 + lo, 8 + hi), r("NM", lo, hi), r("MZ", lo, hi), r("ZP", 7 + lo, 8 + lo) if b else 0.0)
+    cp(r("ZP", 7, 8), r("ZP", W + 7, W + 8))
+    ts(r("SJ"), r("SI"), 2, A.arith_shift_right)
+    cp(r("SQ"), r("SJ"))
+    iota(r("IQ"), [[0, 16], [1, 4]], 0, 0)
+    ts(r("MQ"), r("IQ"), r("SQ"), A.is_equal)
+    ts(r("RS"), r("IQ"), 0.0, A.is_gt)
+    zero(r("WU"))
+    ts(r("BW"), r("BO"), r("WT"), A.mult)
+    for s in range(4):
+        cp(r("WU", 128 * s + s, 128 * s + 128, 4), r("BW", s, 128, 4))
+    sel(r("ID"), r("ON"), [[-1, 128]], A.is_equal, 0, 1)
+    act(r("NI"), r("ID"), F.Copy, 0.0, -1.0)
+    ms(r("CM"), 0.0)
+    for s in range(16):
+        act(r("CM", 128 * s + s, 128 * s + 128, 16), r("BO", 0, 128, 16), F.Copy)
+    cp(r("TH"), r("TI"))
+    ts(r("BIG"), r("SC"), 4.0, A.mult, 4096.0, A.add)
+    ts(r("SB"), r("SC"), -1.0, A.mult, 0.5, A.add)
+    zero(r("DG"))
+    for s in range(4):
+        act(r("DG", 128 * s + s, 128 * s + 128, 4), r("ID", s, 128, 4), F.Copy)
+    sel(r("S1"), r("ON"), [[-1, 128]], A.is_equal, 1, 1)
+    sel(r("S2"), r("ON"), [[-1, 128]], A.is_equal, -15, 1)
+    tt(r("S1"), r("S1"), r("BO"), A.mult)
+    tt(r("S2"), r("S2"), r("BO"), A.mult)
+    tt(r("S2"), r("S2"), r("S1"), A.subtract)
+    tt(r("DB"), r("S2"), r("ID"), A.add)
+    iota(r("JS"), [[0, 8], [1, 16]], 0, 0)
+    ts(r("G1"), r("JS"), r("SC"), A.is_ge, 2.0, A.mult)
+    ts(r("G0"), r("G1"), -1.0, A.add)
+    ts(r("HB"), r("BO"), 0.5, A.mult)
+    zero(r("HL"))
+    for s in range(4):
+        cp(r("HL", 128 * s + s, 128 * s + 128, 4), r("HB", s, 128, 4))
+    iota(r("BR"), [[0, 8], [16, 16]], 0, 0)
+    iota(r("CR"), [[256, 16], [0, 4]], 0, 0)
+    ms(r("OB"), 1.0)
+    ts(r("IH"), r("ID"), 0.5, A.mult)
+    iota(r("T0"), [[16, 16]], W, 0)
+    ts(r("TR"), r("T0"), r("SC"), A.add)
+    ms(r("ZE"), 0.0)
+    for p in range(NPC):
+        ms(r("DU", 0, 1, p=p), 0.0)
+    for b in range(4):
+        cp(r("YO", 512 * b, 512 * b + 512), r("OW", 512 * b, 512 * b + 512))
+
+    SZ = r("ZP", 8, 8 + W)
+
+    def front(t):
+        hb = "hb%d" % t
+        u, zw, za = r("ps4", 0, 64), r("ps4", 64, 128), r("ps4", 128, 384)
+        mm(u, [(r("WU", 128 * s, 128 * s + 128), r(hb, s, P, 4)) for s in range(4)])
+        tt(r("UM"), u, r("MQ"), A.mult)
+        scan(r("US"), r("RS"), r("UM"))
+        cp(r("UI"), r("US", 3, 64, 4))
+        ts(r("UA"), r("UI"), 4095, A.bitwise_and)
+        ts(r("UB"), r("UA"), 32, A.add)
+        tt(r("UP"), r("UA"), r("UB"), A.mult)
+        ts(r("UX"), r("UP"), 5, A.arith_shift_right, 2032, A.bitwise_and)
+        ts(r("LX"), r("UX"), r("SC"), A.add)
+        ts(r("XF"), r("UX"), r("SC"), A.add)
+        for s in range(16):
+            o, i = r("HX", s, 16 * P, 16), r(hb)
+            if HEXP[s] == "a":
+                act(o, i, F.Copy)
+            elif HEXP[s] == "v":
+                cp(o, i)
+            else:
+                sel(o, i, [[0, P]], A.is_gt, 1, 0)
+        gat("v", r("LP"), SZ, r("LX"))
+
+    def before(t):
+        zw, za = r("ps4", 64, 128), r("ps4", 128, 384)
+        gat("a", r("ZA"), SZ, r("LX"))
+        mm(zw, [(r("DG", 128 * s, 128 * s + 128), r("ZA", s, P, 4)) for s in range(4)], x4=4)
+        tt(r("ZM"), zw, r("MQ"), A.mult)
+        scan(r("ZS"), r("RS"), r("ZM"))
+        cp(r("OI"), r("ZS", 3, 64, 4))
+        tt(r("FR"), r("ZS", 3, 64, 4), r("OI"), A.subtract)
+        ts(r("AL"), r("FR"), -4096.0, A.mult, 7.0, A.add)
+        tt(r("AM"), r("AL"), r("XF"), A.add)
+        cp(r("LA"), r("AM"))
+        gat("a", r("ZB"), r("ZP"), r("LA"))
+        act(za, r("ZA"), F.Copy)
+        tt(r("DZ"), r("ZB"), za, A.subtract)
+
+    def rules(t, p):
+        c0, c1 = PIECES[p]
+        nc, nl, q4, L0, L1 = c1 - c0, 16 * (c1 - c0), 4 * (c1 - c0), 16 * c0, 16 * c1
+        b0, b1, b5 = "ps%d" % (2 * p), "ps%d" % (2 * p + 1), "ps5"
+        hb = "hb%d" % t
+        for (l, h) in VCH:
+            gat("v", r("D", 16 * l, 16 * h, p=p), r("HD"), r("LP", L0 + l, L0 + h), r("HX", 16 * (L0 + l), 16 * (L0 + h)),
+                A.subtract)
+            act(r("AB", 16 * l, 16 * h, p=p), r("D", 16 * l, 16 * h, p=p), F.Abs)
+        for k, (l, h) in enumerate(ACH):
+            v, q = r("D", 16 * l, 16 * h, p=p), r("ps%d" % (6 + k % 2), 0, 16 * (h - l))
+            gat("a", v, r("HD"), r("LP", L0 + l, L0 + h))
+            mm(q, [(r("NI"), r("HX", 16 * (L0 + l), 16 * (L0 + h))), (r("ID"), v)])
+            act(r("AB", 16 * l, 16 * h, p=p), q, F.Abs)
+        for (l, h) in NCH:
+            d, y = r(b0, l, h), lambda n: r(n, l, h, p=p)
+            mm(d, [(r("CM", 128 * s, 128 * s + 128), r("AB", 16 * l + s, 16 * h, 16, p=p)) for s in range(16)])
+            ts(y("NA"), d, r("TH"), A.is_lt, r("BIG"), A.mult)
+            tt(y("NX"), y("NA"), d, A.max)
+            ts(y("NN"), y("NX"), 2, A.arith_shift_right, 15, A.bitwise_and)
+            cp(y("NB"), y("NN"))
+        w0, ad = r(b0, 128, 128 + nl), r(b0, 256, 256 + nl)
+        dl, eb, dn = r(b1, 0, nl), r(b1, 128, 128 + nl), r(b1, 256, 256 + nl)
+        ew, fw = r(b5, 256 * p, 256 * p + q4), r(b5, 256 * p + 64, 256 * p + 64 + q4)
+        Y = r("Y", p=p)
+        mm(dl, [(r("DB"), r("NB", p=p))])
+        wrap = lambda: [(r("BR"), r("OB", 0, q4)), (r("OB"), r("CR", 0, q4))] + \
+            [(r("HL", 128 * s, 128 * s + 128), r("Y", s, nl, 4, p=p)) for s in range(4)]
+        for k in range(5):
+            if k:
+                act(r("SG", p=p), eb, F.Sign, r("SB"))
+            if k == 4:
+                act(r("E4", p=p), eb, F.Copy)
+            tt(Y, r("SG", p=p) if k else r("G0", 0, nl), dl, A.mult)
+            mm(eb, [(r("HB"), Y)])
+            if k == 3:
+                mm(ew, wrap())
+                tt(r("EM", p=p), ew, r("MQ", 0, q4), A.mult)
+                scan(r("ES", p=p), r("RS", 0, q4), r("EM", p=p))
+                cp(r("EL", p=p), r("ES", 3, q4, 4, p=p))
+            if k == 4:
+                mm(fw, wrap())
+        ds = r("DS", p=p)
+        gat("a", ds, r("D", p=p), r("EL", p=p))
+        for a, b, m in ((0, VL, "v"), (VL, nl, "a")):
+            if a < b:
+                x, y = r(hb, L0 + a, L0 + b), r("DS", a, b, p=p)
+                mm(r(b0, 256 + a, 256 + b), [(r("ID"), y)] + ([(r("NI"), x)] if m == "a" else []))
+                mm(r(b0, 128 + a, 128 + b), [(r("IH"), y), (r("IH") if m == "a" else r("ID"), x)])
+        act(ad, ad, F.Abs)
+        ts(r("FD", p=p), w0, -0.25, A.add)
+        tt(r("TD", p=p), r("FD", p=p), ad, A.subtract)
+        tt(dn, r("E4", p=p), eb, A.is_equal)
+        tt(r("QD", p=p), r("TD", p=p), dn, A.mult)
+        hn = r("hn", P * t + L0, P * t + L1)
+        tt(hn, r("QD", p=p), ad, A.add)
+        nh, arr = "hb%d" % (t + 1), "ar%d%d" % (t + 1, p)
+        op("g", lambda e: e.remote_dma(T[nh][:, L0:L1], ap(hn), T.sem[arr], T.sem.ls, pid, rid, mask),
+           [hn], [r(nh, L0, L1)], 0.3, sem=(arr, ne), lat=2.5)
+
+    def calls(t, p):
+        c0, c1 = PIECES[p]
+        nc, nl, q4, L0, L1 = c1 - c0, 16 * (c1 - c0), 4 * (c1 - c0), 16 * c0, 16 * c1
+        fw, e4p = r("ps5", 256 * p + 64, 256 * p + 64 + q4), r("ps%d" % (2 * p), 384, 384 + nl)
+        za = r("ps4", 128 + L0, 128 + L1)
+        tt(r("FM", p=p), fw, r("MQ", 0, q4), A.mult)
+        scan(r("FS", p=p), r("RS", 0, q4), r("FM", p=p))
+        tr = r("TR", c0, c1)
+        x = lambda n, a=0, b=0: r(n, a, nc - b, p=p)
+        tt(x("DW"), r("FS", 3, q4, 4, p=p), r("ES", 3, q4, 4, p=p), A.is_equal)
+        tt(x("DT"), x("DW"), tr, A.mult)
+        tt(x("XQ"), x("DT"), r("XF", c0, c1), A.max)
+        tt(x("DU", 1), x("XQ", 1), x("XQ", 0, 1), A.is_equal)
+        tt(x("T2", 2), x("XQ", 2), x("XQ", 0, 2), A.is_equal)
+        tt(x("T3", 3), x("XQ", 3), x("XQ", 0, 3), A.is_equal)
+        tt(x("DU", 2), x("DU", 2), x("T2", 2), A.max)
+        tt(x("DU", 3), x("DU", 3), x("T3", 3), A.max)
+        tt(x("DM"), x("DU"), tr, A.mult)
+        tt(x("DX"), x("DM"), x("XQ"), A.max)
+        cp(x("SL"), x("DX"))
+        ts(e4p, r("E4", p=p), r("SC"), A.is_equal)
+        tt(r("DE", p=p), r("DZ", L0, L1), e4p, A.mult)
+        tt(r("CL", p=p), r("DE", p=p), za, A.add)
+        for c in range(nc - 4, -1, -4):
+            off, col = r("SL", c, c + 4, p=p), r("CL", 16 * c, 16 * c + 64, p=p)
+            dur = 0.05 + 64 * 3.0 * CY
+
+            def sc(w, off=off, col=col):
+                op("v", lambda e: e.tensor_copy(out=ap(w).indirect(ap(off)), in_=ap(col)), [off, col], [w], dur)
+            if t < STEPS - 1:
+                sc(r("MZ"))
+            op("a", lambda e, off=off: e.activation(out=ap(r("NM")).indirect(ap(off)), in_=ap(r("ZE")), func=F.Silu),
+               [off, r("ZE")], [r("NM")], dur + 0.015)
+            sc(r("YO"))
+
+    for t in range(STEPS):
+        front(t)
+        for p in range(NPC):
+            rules(t, p)
+        before(t)
+        for p in range(NPC):
+            calls(t, p)
+        if t < STEPS - 1:
+            scan(SZ, r("NM", 0, W), r("MZ", 0, W))
+            cp(r("ZP", 7, 8), r("ZP", W + 7, W + 8))
+    dma("s", lambda: T.yo[:], lambda: T.YO[:, 0:W], [r("YO", 0, W)], [], 5.0)
+    act(r("YM"), r("NM", 0, W), F.Copy, 1.0, -1.0)
+    dma("s", lambda: T.ym[:], lambda: T.YM[0:128:16, :], [r("YM")], [], 2.0)
+    for p in range(NPC):
+        lo, hi = lanes(p)
+        dma("s", lambda lo=lo, hi=hi: T.yh[:, lo:hi], lambda lo=lo, hi=hi: T["hb%d" % STEPS][:, lo:hi],
+            [r("hb%d" % STEPS, lo, hi)], [], 2.0)
+
+    emit(g, T, ops, eng, ne)
+
+
+def meet(x, y):
+    if x[1] >= y[2] or y[1] >= x[2]:
+        return False
+    return not (x[3] == y[3] and x[3] > 1 and (x[1] - y[1]) % x[3])
+
+
+def covers(x, y):
+    return x[3] == 1 and x[1] <= y[1] and x[2] >= y[2]
+
+
+def emit(g, T, ops, eng, ne):
+    n = len(ops)
+    dep = [dict() for _ in range(n)]
+    hist = {}
+    for i, o in enumerate(ops):
+        for wr, xs in ((False, o["rd"]), (True, o["wr"])):
+            for x in xs:
+                psum = x[0][:2] == "ps"
+                for (j, y, w) in hist.get(x[0], []):
+                    same = ops[j]["q"] == o["q"] and ops[j]["sem"] is None
+                    if (wr or w) and meet(x, y):
+                        wait = (w or not same) and not (same and o["q"] == "p" and w and wr)
+                        dep[i][j] = dep[i].get(j, False) or wait
+                    elif psum:
+                        dep[i][j] = dep[i].get(j, False) or not same
+        for wr, xs in ((False, o["rd"]), (True, o["wr"])):
+            for x in xs:
+                h = hist.setdefault(x[0], [])
+                if wr:
+                    h[:] = [z for z in h if z[0] == i or not covers(x, z[1])]
+                h.append((i, x, wr))
+    succ = [[] for _ in range(n)]
+    for i in range(n):
+        for j in dep[i]:
+            succ[j].append(i)
+    HOP = 0.08
+    tail = [0.0] * n
+    for i in range(n - 1, -1, -1):
+        o = ops[i]
+        tail[i] = o["dur"] + o["lat"] + max([tail[k] + HOP for k in succ[i]], default=0.0)
+    left = [len(dep[i]) for i in range(n)]
+    avail = [0.0] * n
+    ready = {q: [] for q in eng}
+    for i in range(n):
+        if not left[i]:
+            ready[ops[i]["q"]].append(i)
+    free = {q: 0.0 for q in eng}
+    order = []
+    while len(order) < n:
+        t0, q = min((max(free[q], min(avail[i] for i in ready[q])), q) for q in eng if ready[q])
+        i = max((k for k in ready[q] if avail[k] <= t0 + 1e-9), key=lambda k: (tail[k], -k))
+        ready[q].remove(i)
+        o = ops[i]
+        free[q] = t0 + o["dur"]
+        for k in succ[i]:
+            avail[k] = max(avail[k], t0 + o["dur"] + o["lat"] + HOP if dep[k][i] else t0)
+            left[k] -= 1
+            if not left[k]:
+                ready[ops[k]["q"]].append(k)
+        order.append(i)
+    count = {q: 0 for q in eng}
+    mark, know, after, place = {}, {q: {} for q in eng}, {}, {}
+    final = {}
+    for i in order:
+        o = ops[i]
+        q = o["q"]
+        kn = know[q]
+        for j in sorted((j for j in dep[i] if dep[i][j]), key=lambda j: -place[j]):
+            s, v = mark[j]
+            if kn.get(s, 0) >= v:
+                continue
+            eng[q].wait_ge(T.sem[s], v)
+            for s2, v2 in after[j].items():
+                if kn.get(s2, 0) < v2:
+                    kn[s2] = v2
+        ins = o["fn"](eng[q])
+        remote = o["sem"] is not None and o["sem"][0][:2] == "ar"
+        if o["sem"] is None:
+            count[q] += 1
+            mark[i] = ("q" + q, count[q])
+            ins.then_inc(T.sem["q" + q], 1)
+        else:
+            mark[i] = o["sem"]
+            if not remote:
+                ins.then_inc(T.sem[o["sem"][0]], 16)
+        final[mark[i][0]] = mark[i][1]
+        after[i] = {} if remote else dict(kn)
+        after[i][mark[i][0]] = mark[i][1]
+        place[i] = len(place)
+    for s, v in final.items():
+        g.wait_ge(T.sem[s], v)
+    g.wait_ge(T.sem.ls, ne * STEPS * NPC)

@@ -1,70 +1,39 @@
 from concourse.mybir import AluOpType as A, ActivationFunctionType as F
 
 N, STEPS, W, R, P = 4, 4, 2048, 4096, 256
-PIECES = [(8, 16), (0, 8)]
+PIECES = [(12, 16, "v", 64), (8, 12, "a", 32), (4, 8, "v", 64), (0, 4, "v", 32)]
+GROUPS = [(0, 1), (2, 3)]
 NPC = len(PIECES)
-VCH = [(0, 32), (32, 64)]
-ACH = [(64, 96), (96, 128)]
-NCH = [(0, 64), (64, 128)]
-VL = 64
 TW = W + P
-HEXP = "agavaagavaagavag"
+HEXP = "vvvgvavgvvvgvavg"
 
 SCRATCH = {
     "HD": ("sbuf", [128, R], "bfloat16"), "OW": ("sbuf", [128, W], "int32"), "MK": ("sbuf", [128, 128], "int32"),
     "MB": ("sbuf", [128, 128], "bfloat16"), "WT": ("sbuf", [128, 1], "bfloat16"), "TI": ("sbuf", [128, 1], "int32"),
-    "YO": ("sbuf", [128, TW], "float32"), "MZ": ("sbuf", [128, TW], "float32"), "NM": ("sbuf", [128, TW], "float32"),
+    "YO": ("sbuf", [128, W], "float32"), "MZ": ("sbuf", [128, TW], "float32"), "NM": ("sbuf", [128, TW], "float32"),
     "ZP": ("sbuf", [128, W + 8], "float32"), "YM": ("sbuf", [128, W], "float32"),
-    "PI": ("sbuf", [128, 1], "int32"), "SI": ("sbuf", [128, 1], "int32"), "SJ": ("sbuf", [128, 1], "int32"),
-    "SC": ("sbuf", [128, 1], "float32"), "SQ": ("sbuf", [128, 1], "float32"), "TH": ("sbuf", [128, 1], "float32"),
-    "BIG": ("sbuf", [128, 1], "float32"), "SB": ("sbuf", [128, 1], "float32"),
-    "ON": ("sbuf", [128, 128], "bfloat16"), "B1": ("sbuf", [128, 128], "bfloat16"), "BO": ("sbuf", [128, 128], "bfloat16"),
-    "HB": ("sbuf", [128, 128], "bfloat16"), "ID": ("sbuf", [128, 128], "bfloat16"), "IH": ("sbuf", [128, 128], "bfloat16"),
-    "NI": ("sbuf", [128, 128], "bfloat16"),
-    "S1": ("sbuf", [128, 128], "bfloat16"), "S2": ("sbuf", [128, 128], "bfloat16"), "DB": ("sbuf", [128, 128], "bfloat16"),
-    "IK": ("sbuf", [128, 16], "float32"), "OH": ("sbuf", [128, 16], "float32"),
-    "CM": ("sbuf", [128, 2048], "bfloat16"), "SR": ("sbuf", [128, 2048], "bfloat16"), "BW": ("sbuf", [128, 128], "bfloat16"),
-    "WU": ("sbuf", [128, 512], "bfloat16"), "HL": ("sbuf", [128, 512], "bfloat16"), "DG": ("sbuf", [128, 512], "float32"),
-    "IQ": ("sbuf", [128, 64], "float32"), "MQ": ("sbuf", [128, 64], "float32"), "RS": ("sbuf", [128, 64], "float32"),
-    "JS": ("sbuf", [128, 128], "float32"), "G1": ("sbuf", [128, 128], "float32"), "G0": ("sbuf", [128, 128], "bfloat16"),
-    "T0": ("sbuf", [128, 16], "float32"), "TR": ("sbuf", [128, 16], "float32"),
-    "BR": ("sbuf", [1, 128], "bfloat16"), "OB": ("sbuf", [1, 128], "bfloat16"), "CR": ("sbuf", [1, 64], "bfloat16"),
-    "ZE": ("sbuf", [128, 64], "float32"),
-    "LP": ("sbuf", [128, P], "uint16"), "ZA": ("sbuf", [128, P], "float32"), "ZB": ("sbuf", [128, P], "float32"),
-    "DZ": ("sbuf", [128, P], "float32"), "HX": ("sbuf", [128, 16 * P], "bfloat16"), "hn": ("sbuf", [128, P * STEPS], "bfloat16"),
+    "CM": ("sbuf", [128, 2048], "bfloat16"), "SR": ("sbuf", [128, 2048], "bfloat16"),
+    "BA": ("sbuf", [2, 128], "bfloat16"), "BR": ("sbuf", [2, 128], "bfloat16"),
+    "CA": ("sbuf", [2, 64], "bfloat16"), "CR": ("sbuf", [2, 64], "bfloat16"),
+    "HX": ("sbuf", [128, 16 * P], "bfloat16"), "AB": ("sbuf", [128, 16 * P], "bfloat16"),
 }
+for _d, _w, _ns in (("float32", 1, "SC SQ TH BIG SB KB"), ("int32", 1, "PI SI SJ"),
+                    ("bfloat16", 128, "ON B1 BO HB ID IH NI S1 S2 DB BW G0"),
+                    ("float32", 16, "IK OH T0 TR XF FR AL AM DW DT XQ DU T2 T3 DM DX"), ("int32", 16, "UI UA UB UP UX OI"),
+                    ("uint16", 16, "LX LA SL EL"), ("bfloat16", 512, "WU HL"), ("float32", 512, "DG"),
+                    ("float32", 64, "IQ MQ RS ZE UM US ZM ZS EM ES FM FS"), ("float32", 128, "JS G1"),
+                    ("float32", P, "ZA ZB DZ NA DE"), ("int32", P, "NX NN FD CL"), ("uint16", P, "LP"),
+                    ("bfloat16", P, "NB Y SG E4 DS TD QD")):
+    for _n in _ns.split():
+        SCRATCH[_n] = ("sbuf", [128, _w], _d)
 for _b in range(8):
     SCRATCH["ps%d" % _b] = ("psum", [128, 512], "float32")
 for _t in range(STEPS + 1):
     SCRATCH["hb%d" % _t] = ("sbuf", [128, P], "bfloat16")
-_WIDE = {
-    "D": (16, "bfloat16"), "AB": (16, "bfloat16"), "NA": (1, "float32"), "NX": (1, "int32"), "NN": (1, "int32"),
-    "NB": (1, "bfloat16"), "Y": (1, "bfloat16"), "SG": (1, "bfloat16"), "E4": (1, "bfloat16"), "DS": (1, "bfloat16"),
-    "FD": (1, "int32"), "TD": (1, "bfloat16"), "QD": (1, "bfloat16"), "DE": (1, "float32"), "CL": (1, "int32"),
-}
-_SMALL = {"EL": "uint16", "DW": "float32", "DT": "float32", "XQ": "float32", "DU": "float32", "T2": "float32",
-          "T3": "float32", "DM": "float32", "DX": "float32", "SL": "uint16"}
-_QUAD = ["EM", "ES", "FM", "FS"]
-PLACE = {}
-for _p, (_c0, _c1) in enumerate(PIECES):
-    _nc = _c1 - _c0
-    for _n, (_k, _d) in _WIDE.items():
-        SCRATCH["%s%d" % (_n, _p)] = ("sbuf", [128, _k * 16 * _nc], _d)
-        PLACE[_n, _p] = ("%s%d" % (_n, _p), 0, _k * 16 * _nc)
-_fill = {}
-for _p, _ns in [(k, list(_SMALL.items()) + [(n, "float32") for n in _QUAD]) for k in range(NPC)] + [(None, [
-        ("UM", "float32"), ("US", "float32"), ("ZM", "float32"), ("ZS", "float32"), ("UI", "int32"), ("UA", "int32"),
-        ("UB", "int32"), ("UP", "int32"), ("UX", "int32"), ("XF", "float32"), ("LX", "uint16"), ("OI", "int32"),
-        ("FR", "float32"), ("AL", "float32"), ("AM", "float32"), ("LA", "uint16")])]:
-    _nc = 16 if _p is None else PIECES[_p][1] - PIECES[_p][0]
-    for _n, _d in _ns:
-        _w = 4 * _nc if _n in _QUAD + ["UM", "US", "ZM", "ZS"] else _nc
-        PLACE[_n, _p] = ("sm_" + _d, _fill.get(_d, 0), _w)
-        _fill[_d] = _fill.get(_d, 0) + -(-_w // 16) * 16
-for _d, _w in _fill.items():
-    SCRATCH["sm_" + _d] = ("sbuf", [128, _w], _d)
-SEMAPHORES = ["qv", "qa", "qp", "qg", "ls"] + ["dm%d" % k for k in range(24)] + \
-    ["ar%d%d" % (t, p) for t in range(1, STEPS + 1) for p in range(NPC)]
+    SCRATCH["hn%d" % _t] = ("sbuf", [128, P], "bfloat16")
+for _p in range(NPC):
+    SCRATCH["D%d" % _p] = ("sbuf", [128, 256 * (PIECES[_p][1] - PIECES[_p][0])], "bfloat16")
+SEMAPHORES = ["qv", "qa", "qp", "qg", "ls"] + ["dm%d" % k for k in range(24)] + ["ar%d" % t for t in range(1, STEPS + 1)]
 
 
 def rank_program(g, core, T, topo):
@@ -77,18 +46,17 @@ def rank_program(g, core, T, topo):
     ne = len(topo.engines(core, dst))
     eng = {"v": g.vector, "a": g.scalar, "p": g.tensor, "g": g, "s": g.sync}
     CY = 1.0e-3
-    ops = []
+    ops, pr = [], [0.0]
 
-    def r(n, lo=None, hi=None, st=1, p=None):
-        b, o, w = PLACE[n, p] if (n, p) in PLACE else (n, 0, SCRATCH[n][1][1])
-        return (b, o + (0 if lo is None else lo), o + (w if hi is None else hi), st)
+    def r(n, lo=0, hi=None, st=1):
+        return (n, lo, SCRATCH[n][1][1] if hi is None else hi, st)
 
     def ap(x):
         if not isinstance(x, tuple):
             return x
         b, lo, hi, st = x
-        if SCRATCH[b][1][0] == 1:
-            return T[b][0:1, lo:hi]
+        if SCRATCH[b][1][0] == 2:
+            return T[b][0:2, lo:hi]
         return T[b][:, lo:hi] if st == 1 else T[b][:, lo:hi:st]
 
     def cnt(x):
@@ -102,7 +70,7 @@ def rank_program(g, core, T, topo):
 
     def op(q, fn, rd, wr, dur, sem=None, lat=0.0):
         ops.append({"q": q, "fn": fn, "rd": [x for x in rd if isinstance(x, tuple)], "wr": wr, "dur": dur,
-                    "sem": sem, "lat": lat})
+                    "sem": sem, "lat": lat, "pr": pr[0]})
 
     def tt(o, a, b, f):
         c = cnt(o) * (1 if ps(a) or ps(b) else 2)
@@ -120,8 +88,8 @@ def rank_program(g, core, T, topo):
         c = cnt(o) * (0.5 if two(o, a) else 1)
         op("v", lambda e: e.tensor_copy(out=ap(o), in_=ap(a)), [a], [o], max(64, c) * CY)
 
-    def scan(o, a, b, ini=0.0):
-        op("v", lambda e: e.tensor_tensor_scan(out=ap(o), data0=ap(a), data1=ap(b), initial=ap(ini), op0=A.mult, op1=A.add),
+    def scan(o, a, b, ini=0.0, o0=A.mult, o1=A.add):
+        op("v", lambda e: e.tensor_tensor_scan(out=ap(o), data0=ap(a), data1=ap(b), initial=ap(ini), op0=o0, op1=o1),
            [a, b, ini], [o], max(64, cnt(o)) * CY)
 
     def ms(o, k):
@@ -131,14 +99,16 @@ def rank_program(g, core, T, topo):
         op("a", lambda e: e.activation(out=ap(o), in_=ap(a), func=f, bias=ap(bias), scale=ap(scale)), [a, bias, scale], [o],
            max(64, cnt(o)) * CY + 0.03)
 
-    def gat(q, o, w, off, in1=None, f=None):
+    def gat(q, o, w, off, in1=None):
         d = 0.05 + 1.5 * cnt(o) * CY
         if q == "a":
             op("a", lambda e: e.activation(out=ap(o), in_=ap(w).indirect(ap(off)), func=F.Copy), [w, off], [o], d + 0.015)
         elif in1 is None:
-            op("v", lambda e: e.tensor_copy(out=ap(o), in_=ap(w).indirect(ap(off))), [w, off], [o], d)
+            op("v", lambda e: e.tensor_scalar(out=ap(o), in0=ap(w).indirect(ap(off)), scalar1=-1.0, scalar2=None, op0=A.mult),
+               [w, off], [o], d)
         else:
-            op("v", lambda e: e.tensor_tensor(out=ap(o), in0=ap(w).indirect(ap(off)), in1=ap(in1), op=f), [w, off, in1], [o], d)
+            op("v", lambda e: e.tensor_tensor(out=ap(o), in0=ap(w).indirect(ap(off)), in1=ap(in1), op=A.subtract),
+               [w, off, in1], [o], d)
 
     def mm(o, pairs, x4=1):
         def fn(e):
@@ -155,9 +125,6 @@ def rank_program(g, core, T, topo):
         ndma[0] += 1
         op(q, lambda e: e.dma_start(out=o_fn(), in_=i_fn()), rd, wr, 0.1, sem=(s, 16), lat=dur)
 
-    def lanes(p):
-        return 16 * PIECES[p][0], 16 * PIECES[p][1]
-
     dma("s", lambda: T.MK[:], lambda: T.marks[:], [], [r("MK")], 2.0)
     dma("a", lambda: T.hb0[:], lambda: T.h0[:], [], [r("hb0")], 2.0)
     for b in range(4):
@@ -171,11 +138,8 @@ def rank_program(g, core, T, topo):
         op("g", lambda e: e.iota(ap(o), pat, base, cm, allow_small_or_imprecise_dtypes=True), [], [o],
            0.13 + 2 * cnt(o) * CY)
 
-    def zero(o):
-        iota(o, [[0, cnt(o)]], 0, 0)
-
-    def sel(o, a, pat, f, base, cm):
-        op("g", lambda e: e.affine_select(out=ap(o), in_=ap(a), pattern=pat, compare_op=f, fill=0.0, base=base,
+    def sel(o, a, pat, f, base, cm, fill=0.0):
+        op("g", lambda e: e.affine_select(out=ap(o), in_=ap(a), pattern=pat, compare_op=f, fill=fill, base=base,
                                           channel_multiplier=cm), [a], [o], 0.17 + 2 * cnt(o) * CY)
     iota(r("PI"), [[0, 1]], 0, 1)
     ms(r("ON"), 1.0)
@@ -194,30 +158,30 @@ def rank_program(g, core, T, topo):
         for k in range(4 * b, 4 * b + 4):
             mm(r("ps%d" % b, 128 * (k % 4), 128 * (k % 4) + 128), [(r("SR", 128 * k, 128 * k + 128), r("MB"))])
         m, n2 = r("ps%d" % b), r("ps%d" % (4 + b))
-        act(n2, m, F.Copy, 1 / 4096, -1 / 4096)
-        act(r("NM", lo, hi), m, F.Copy, 1.0, -1.0)
-        tt(r("MZ", lo, hi), r("OW", lo, hi), m, A.mult)
-        tt(r("MZ", lo, hi), r("MZ", lo, hi), n2, A.add)
-        scan(r("ZP", 8 + lo, 8 + hi), r("NM", lo, hi), r("MZ", lo, hi), r("ZP", 7 + lo, 8 + lo) if b else 0.0)
+        act(n2, m, F.Copy, 8192.0, -8192.0)
+        act(r("NM", lo, hi), m, F.Copy, -1 / 4096, 8192.0)
+        tt(r("MZ", lo, hi), n2, r("OW", lo, hi), A.subtract)
+        scan(r("ZP", 8 + lo, 8 + hi), r("NM", lo, hi), r("MZ", lo, hi), r("ZP", 7 + lo, 8 + lo) if b else 0.0, A.add, A.min)
     cp(r("ZP", 7, 8), r("ZP", W + 7, W + 8))
+    for n in ("WU", "DG", "HL"):
+        ms(r(n), 0.0)
+    for k in range(4):
+        ms(r("CM", 512 * k, 512 * k + 512), 0.0)
     ts(r("SJ"), r("SI"), 2, A.arith_shift_right)
     cp(r("SQ"), r("SJ"))
     iota(r("IQ"), [[0, 16], [1, 4]], 0, 0)
     ts(r("MQ"), r("IQ"), r("SQ"), A.is_equal)
     ts(r("RS"), r("IQ"), 0.0, A.is_gt)
-    zero(r("WU"))
     ts(r("BW"), r("BO"), r("WT"), A.mult)
     for s in range(4):
         cp(r("WU", 128 * s + s, 128 * s + 128, 4), r("BW", s, 128, 4))
     sel(r("ID"), r("ON"), [[-1, 128]], A.is_equal, 0, 1)
     act(r("NI"), r("ID"), F.Copy, 0.0, -1.0)
-    ms(r("CM"), 0.0)
     for s in range(16):
         act(r("CM", 128 * s + s, 128 * s + 128, 16), r("BO", 0, 128, 16), F.Copy)
     cp(r("TH"), r("TI"))
     ts(r("BIG"), r("SC"), 4.0, A.mult, 4096.0, A.add)
     ts(r("SB"), r("SC"), -1.0, A.mult, 0.5, A.add)
-    zero(r("DG"))
     for s in range(4):
         act(r("DG", 128 * s + s, 128 * s + 128, 4), r("ID", s, 128, 4), F.Copy)
     sel(r("S1"), r("ON"), [[-1, 128]], A.is_equal, 1, 1)
@@ -230,26 +194,25 @@ def rank_program(g, core, T, topo):
     ts(r("G1"), r("JS"), r("SC"), A.is_ge, 2.0, A.mult)
     ts(r("G0"), r("G1"), -1.0, A.add)
     ts(r("HB"), r("BO"), 0.5, A.mult)
-    zero(r("HL"))
     for s in range(4):
         cp(r("HL", 128 * s + s, 128 * s + 128, 4), r("HB", s, 128, 4))
-    iota(r("BR"), [[0, 8], [16, 16]], 0, 0)
-    iota(r("CR"), [[256, 16], [0, 4]], 0, 0)
-    ms(r("OB"), 1.0)
+    iota(r("BA"), [[0, 8], [16, 16]], 0, 0)
+    sel(r("BR"), r("BA"), [[0, 128]], A.is_equal, 0, 1, 1.0)
+    iota(r("CA"), [[0, 4], [256, 4], [0, 4]], 0, 0)
+    sel(r("CR"), r("CA"), [[0, 64]], A.not_equal, 0, 1, 1.0)
     ts(r("IH"), r("ID"), 0.5, A.mult)
     iota(r("T0"), [[16, 16]], W, 0)
     ts(r("TR"), r("T0"), r("SC"), A.add)
-    ms(r("ZE"), 0.0)
-    for p in range(NPC):
-        ms(r("DU", 0, 1, p=p), 0.0)
-    for b in range(4):
-        cp(r("YO", 512 * b, 512 * b + 512), r("OW", 512 * b, 512 * b + 512))
+    ms(r("ZE"), 8192.0)
+    ms(r("KB"), 8192.0)
+    for ks in GROUPS:
+        c0 = min(PIECES[k][0] for k in ks)
+        ms(r("DU", c0, c0 + 1), 0.0)
 
     SZ = r("ZP", 8, 8 + W)
 
     def front(t):
-        hb = "hb%d" % t
-        u, zw, za = r("ps4", 0, 64), r("ps4", 64, 128), r("ps4", 128, 384)
+        hb, u = "hb%d" % t, r("ps4", 0, 64)
         mm(u, [(r("WU", 128 * s, 128 * s + 128), r(hb, s, P, 4)) for s in range(4)])
         tt(r("UM"), u, r("MQ"), A.mult)
         scan(r("US"), r("RS"), r("UM"))
@@ -278,125 +241,124 @@ def rank_program(g, core, T, topo):
         scan(r("ZS"), r("RS"), r("ZM"))
         cp(r("OI"), r("ZS", 3, 64, 4))
         tt(r("FR"), r("ZS", 3, 64, 4), r("OI"), A.subtract)
-        ts(r("AL"), r("FR"), -4096.0, A.mult, 7.0, A.add)
+        ts(r("AL"), r("FR"), 4096.0, A.mult, 7.0, A.add)
         tt(r("AM"), r("AL"), r("XF"), A.add)
         cp(r("LA"), r("AM"))
         gat("a", r("ZB"), r("ZP"), r("LA"))
         act(za, r("ZA"), F.Copy)
         tt(r("DZ"), r("ZB"), za, A.subtract)
 
+    def wrap(c0, c1):
+        return [(r("BR"), r("CR", 0, 4 * (c1 - c0)))] + \
+            [(r("HL", 128 * s, 128 * s + 128), r("Y", 16 * c0 + s, 16 * c1, 4)) for s in range(4)]
+
     def rules(t, p):
-        c0, c1 = PIECES[p]
-        nc, nl, q4, L0, L1 = c1 - c0, 16 * (c1 - c0), 4 * (c1 - c0), 16 * c0, 16 * c1
-        b0, b1, b5 = "ps%d" % (2 * p), "ps%d" % (2 * p + 1), "ps5"
-        hb = "hb%d" % t
-        for (l, h) in VCH:
-            gat("v", r("D", 16 * l, 16 * h, p=p), r("HD"), r("LP", L0 + l, L0 + h), r("HX", 16 * (L0 + l), 16 * (L0 + h)),
-                A.subtract)
-            act(r("AB", 16 * l, 16 * h, p=p), r("D", 16 * l, 16 * h, p=p), F.Abs)
-        for k, (l, h) in enumerate(ACH):
-            v, q = r("D", 16 * l, 16 * h, p=p), r("ps%d" % (6 + k % 2), 0, 16 * (h - l))
-            gat("a", v, r("HD"), r("LP", L0 + l, L0 + h))
-            mm(q, [(r("NI"), r("HX", 16 * (L0 + l), 16 * (L0 + h))), (r("ID"), v)])
-            act(r("AB", 16 * l, 16 * h, p=p), q, F.Abs)
-        for (l, h) in NCH:
-            d, y = r(b0, l, h), lambda n: r(n, l, h, p=p)
-            mm(d, [(r("CM", 128 * s, 128 * s + 128), r("AB", 16 * l + s, 16 * h, 16, p=p)) for s in range(16)])
-            ts(y("NA"), d, r("TH"), A.is_lt, r("BIG"), A.mult)
-            tt(y("NX"), y("NA"), d, A.max)
-            ts(y("NN"), y("NX"), 2, A.arith_shift_right, 15, A.bitwise_and)
-            cp(y("NB"), y("NN"))
-        w0, ad = r(b0, 128, 128 + nl), r(b0, 256, 256 + nl)
-        dl, eb, dn = r(b1, 0, nl), r(b1, 128, 128 + nl), r(b1, 256, 256 + nl)
-        ew, fw = r(b5, 256 * p, 256 * p + q4), r(b5, 256 * p + 64, 256 * p + 64 + q4)
-        Y = r("Y", p=p)
-        mm(dl, [(r("DB"), r("NB", p=p))])
-        wrap = lambda: [(r("BR"), r("OB", 0, q4)), (r("OB"), r("CR", 0, q4))] + \
-            [(r("HL", 128 * s, 128 * s + 128), r("Y", s, nl, 4, p=p)) for s in range(4)]
+        c0, c1, q, ck = PIECES[p]
+        nl, q4, L0, L1 = 16 * (c1 - c0), 4 * (c1 - c0), 16 * c0, 16 * c1
+        hb, D, bk = "hb%d" % t, "D%d" % p, "ps%d" % p
+        for l in range(0, nl, ck):
+            v = r(D, 16 * l, 16 * (l + ck))
+            lp, hx, ab = r("LP", L0 + l, L0 + l + ck), r("HX", 16 * (L0 + l), 16 * (L0 + l + ck)), \
+                r("AB", 16 * (L0 + l), 16 * (L0 + l + ck))
+            if q == "v":
+                gat("v", v, r("HD"), lp, hx)
+                act(ab, v, F.Abs)
+            else:
+                df = r("ps%d" % (6 + (l // ck) % 2), 0, 16 * ck)
+                gat("a", v, r("HD"), lp)
+                mm(df, [(r("NI"), hx), (r("ID"), v)])
+                act(ab, df, F.Abs)
+        d, w0, ad, dl, eb, dn = [r(bk, 64 * k, 64 * k + nl) for k in range(6)]
+        ew = r(bk, 448, 448 + q4)
+        x = lambda n: r(n, L0, L1)
+        y = lambda n, st=1: r(n, 4 * c0 + st - 1, 4 * c1, st)
+        mm(d, [(r("CM", 128 * s, 128 * s + 128), r("AB", 16 * L0 + s, 16 * L1, 16)) for s in range(16)])
+        ts(x("NA"), d, r("TH"), A.is_lt, r("BIG"), A.mult)
+        tt(x("NX"), x("NA"), d, A.max)
+        ts(x("NN"), x("NX"), 2, A.arith_shift_right, 15, A.bitwise_and)
+        cp(x("NB"), x("NN"))
+        mm(dl, [(r("DB"), x("NB"))])
         for k in range(5):
             if k:
-                act(r("SG", p=p), eb, F.Sign, r("SB"))
+                act(x("SG"), eb, F.Sign, r("SB"))
             if k == 4:
-                act(r("E4", p=p), eb, F.Copy)
-            tt(Y, r("SG", p=p) if k else r("G0", 0, nl), dl, A.mult)
-            mm(eb, [(r("HB"), Y)])
+                act(x("E4"), eb, F.Copy)
+            tt(x("Y"), x("SG") if k else r("G0", 0, nl), dl, A.mult)
+            mm(eb, [(r("HB"), x("Y"))])
             if k == 3:
-                mm(ew, wrap())
-                tt(r("EM", p=p), ew, r("MQ", 0, q4), A.mult)
-                scan(r("ES", p=p), r("RS", 0, q4), r("EM", p=p))
-                cp(r("EL", p=p), r("ES", 3, q4, 4, p=p))
-            if k == 4:
-                mm(fw, wrap())
-        ds = r("DS", p=p)
-        gat("a", ds, r("D", p=p), r("EL", p=p))
-        for a, b, m in ((0, VL, "v"), (VL, nl, "a")):
-            if a < b:
-                x, y = r(hb, L0 + a, L0 + b), r("DS", a, b, p=p)
-                mm(r(b0, 256 + a, 256 + b), [(r("ID"), y)] + ([(r("NI"), x)] if m == "a" else []))
-                mm(r(b0, 128 + a, 128 + b), [(r("IH"), y), (r("IH") if m == "a" else r("ID"), x)])
-        act(ad, ad, F.Abs)
-        ts(r("FD", p=p), w0, -0.25, A.add)
-        tt(r("TD", p=p), r("FD", p=p), ad, A.subtract)
-        tt(dn, r("E4", p=p), eb, A.is_equal)
-        tt(r("QD", p=p), r("TD", p=p), dn, A.mult)
-        hn = r("hn", P * t + L0, P * t + L1)
-        tt(hn, r("QD", p=p), ad, A.add)
-        nh, arr = "hb%d" % (t + 1), "ar%d%d" % (t + 1, p)
-        op("g", lambda e: e.remote_dma(T[nh][:, L0:L1], ap(hn), T.sem[arr], T.sem.ls, pid, rid, mask),
-           [hn], [r(nh, L0, L1)], 0.3, sem=(arr, ne), lat=2.5)
+                mm(ew, wrap(c0, c1))
+                tt(y("EM"), ew, y("MQ"), A.mult)
+                scan(y("ES"), y("RS"), y("EM"))
+                cp(r("EL", c0, c1), y("ES", 4))
+        gat("a", x("DS"), r(D), r("EL", c0, c1))
+        if q == "a":
+            mm(ad, [(r("ID"), x("DS")), (r("NI"), x(hb))])
+        act(ad, ad if q == "a" else x("DS"), F.Abs)
+        mm(w0, [(r("IH"), x("DS")), (r("IH") if q == "a" else r("ID"), x(hb))])
+        ts(x("FD"), w0, -0.25, A.add)
+        tt(x("TD"), x("FD"), ad, A.subtract)
+        tt(dn, x("E4"), eb, A.is_equal)
+        tt(x("QD"), x("TD"), dn, A.mult)
+        tt(x("hn%d" % t), x("QD"), ad, A.add)
 
-    def calls(t, p):
-        c0, c1 = PIECES[p]
-        nc, nl, q4, L0, L1 = c1 - c0, 16 * (c1 - c0), 4 * (c1 - c0), 16 * c0, 16 * c1
-        fw, e4p = r("ps5", 256 * p + 64, 256 * p + 64 + q4), r("ps%d" % (2 * p), 384, 384 + nl)
-        za = r("ps4", 128 + L0, 128 + L1)
-        tt(r("FM", p=p), fw, r("MQ", 0, q4), A.mult)
-        scan(r("FS", p=p), r("RS", 0, q4), r("FM", p=p))
-        tr = r("TR", c0, c1)
-        x = lambda n, a=0, b=0: r(n, a, nc - b, p=p)
-        tt(x("DW"), r("FS", 3, q4, 4, p=p), r("ES", 3, q4, 4, p=p), A.is_equal)
-        tt(x("DT"), x("DW"), tr, A.mult)
-        tt(x("XQ"), x("DT"), r("XF", c0, c1), A.max)
+    def send(t):
+        nh, hn, arr = "hb%d" % (t + 1), r("hn%d" % t), "ar%d" % (t + 1)
+        op("g", lambda e: e.remote_dma(T[nh][:], ap(hn), T.sem[arr], T.sem.ls, pid, rid, mask),
+           [hn], [r(nh)], 1.5, sem=(arr, ne), lat=2.0)
+
+    def calls(t, ks):
+        c0, c1 = min(PIECES[k][0] for k in ks), max(PIECES[k][1] for k in ks)
+        L0, L1 = 16 * c0, 16 * c1
+        e4p, za = r("ps4", 384, 384 + L1 - L0), r("ps4", 128 + L0, 128 + L1)
+        y = lambda n, st=1: r(n, 4 * c0 + st - 1, 4 * c1, st)
+        x = lambda n, a=0, b=0: r(n, c0 + a, c1 - b)
+        z = lambda n: r(n, L0, L1)
+        fw = r("ps5", 4 * c0, 4 * c1)
+        mm(fw, wrap(c0, c1))
+        tt(y("FM"), fw, y("MQ"), A.mult)
+        scan(y("FS"), y("RS"), y("FM"))
+        tt(x("DW"), y("FS", 4), y("ES", 4), A.is_equal)
+        tt(x("DT"), x("DW"), x("TR"), A.mult)
+        tt(x("XQ"), x("DT"), x("XF"), A.max)
         tt(x("DU", 1), x("XQ", 1), x("XQ", 0, 1), A.is_equal)
         tt(x("T2", 2), x("XQ", 2), x("XQ", 0, 2), A.is_equal)
         tt(x("T3", 3), x("XQ", 3), x("XQ", 0, 3), A.is_equal)
         tt(x("DU", 2), x("DU", 2), x("T2", 2), A.max)
         tt(x("DU", 3), x("DU", 3), x("T3", 3), A.max)
-        tt(x("DM"), x("DU"), tr, A.mult)
+        tt(x("DM"), x("DU"), x("TR"), A.mult)
         tt(x("DX"), x("DM"), x("XQ"), A.max)
         cp(x("SL"), x("DX"))
-        ts(e4p, r("E4", p=p), r("SC"), A.is_equal)
-        tt(r("DE", p=p), r("DZ", L0, L1), e4p, A.mult)
-        tt(r("CL", p=p), r("DE", p=p), za, A.add)
-        for c in range(nc - 4, -1, -4):
-            off, col = r("SL", c, c + 4, p=p), r("CL", 16 * c, 16 * c + 64, p=p)
-            dur = 0.05 + 64 * 3.0 * CY
-
-            def sc(w, off=off, col=col):
-                op("v", lambda e: e.tensor_copy(out=ap(w).indirect(ap(off)), in_=ap(col)), [off, col], [w], dur)
-            if t < STEPS - 1:
-                sc(r("MZ"))
+        ts(e4p, z("E4"), r("SC"), A.is_equal)
+        tt(z("DE"), z("DZ"), e4p, A.mult)
+        tt(z("CL"), z("DE"), za, A.add)
+        for c in range(c1 - 4, c0 - 1, -4):
+            off, col = r("SL", c, c + 4), r("CL", 16 * c, 16 * c + 64)
+            op("v", lambda e, off=off, col=col: e.tensor_copy(out=ap(r("MZ")).indirect(ap(off)), in_=ap(col)),
+               [off, col], [r("MZ")], 0.05 + 64 * 3.0 * CY)
             op("a", lambda e, off=off: e.activation(out=ap(r("NM")).indirect(ap(off)), in_=ap(r("ZE")), func=F.Silu),
-               [off, r("ZE")], [r("NM")], dur + 0.015)
-            sc(r("YO"))
+               [off, r("ZE")], [r("NM")], 0.065 + 64 * 3.0 * CY)
 
     for t in range(STEPS):
         front(t)
         for p in range(NPC):
+            pr[0] = 1.0 * (NPC - 1 - p)
             rules(t, p)
+        send(t)
+        pr[0] = 0.0
         before(t)
-        for p in range(NPC):
-            calls(t, p)
+        for ks in GROUPS:
+            calls(t, ks)
         if t < STEPS - 1:
-            scan(SZ, r("NM", 0, W), r("MZ", 0, W))
+            scan(SZ, r("NM", 0, W), r("MZ", 0, W), 0.0, A.add, A.min)
             cp(r("ZP", 7, 8), r("ZP", W + 7, W + 8))
-    dma("s", lambda: T.yo[:], lambda: T.YO[:, 0:W], [r("YO", 0, W)], [], 5.0)
-    act(r("YM"), r("NM", 0, W), F.Copy, 1.0, -1.0)
+    for b in range(4):
+        lo, hi, m = 512 * b, 512 * b + 512, r("ps%d" % b)
+        act(m, r("NM", lo, hi), F.Relu, r("KB"), -2.0)
+        tt(r("YO", lo, hi), m, r("MZ", lo, hi), A.subtract)
+        dma("s", lambda lo=lo, hi=hi: T.yo[:, lo:hi], lambda lo=lo, hi=hi: T.YO[:, lo:hi], [r("YO", lo, hi)], [], 5.0)
+        act(r("YM", lo, hi), m, F.Copy, 1.0, -1 / 8192)
     dma("s", lambda: T.ym[:], lambda: T.YM[0:128:16, :], [r("YM")], [], 2.0)
-    for p in range(NPC):
-        lo, hi = lanes(p)
-        dma("s", lambda lo=lo, hi=hi: T.yh[:, lo:hi], lambda lo=lo, hi=hi: T["hb%d" % STEPS][:, lo:hi],
-            [r("hb%d" % STEPS, lo, hi)], [], 2.0)
+    dma("s", lambda: T.yh[:], lambda: T["hb%d" % STEPS][:], [r("hb%d" % STEPS)], [], 2.0)
 
     emit(g, T, ops, eng, ne)
 
@@ -436,7 +398,7 @@ def emit(g, T, ops, eng, ne):
     for i in range(n):
         for j in dep[i]:
             succ[j].append(i)
-    HOP = 0.08
+    HOP = 0.1
     tail = [0.0] * n
     for i in range(n - 1, -1, -1):
         o = ops[i]
@@ -451,7 +413,7 @@ def emit(g, T, ops, eng, ne):
     order = []
     while len(order) < n:
         t0, q = min((max(free[q], min(avail[i] for i in ready[q])), q) for q in eng if ready[q])
-        i = max((k for k in ready[q] if avail[k] <= t0 + 1e-9), key=lambda k: (tail[k], -k))
+        i = max((k for k in ready[q] if avail[k] <= t0 + 1e-9), key=lambda k: (tail[k] + ops[k]["pr"], -k))
         ready[q].remove(i)
         o = ops[i]
         free[q] = t0 + o["dur"]
@@ -492,4 +454,4 @@ def emit(g, T, ops, eng, ne):
         place[i] = len(place)
     for s, v in final.items():
         g.wait_ge(T.sem[s], v)
-    g.wait_ge(T.sem.ls, ne * STEPS * NPC)
+    g.wait_ge(T.sem.ls, ne * STEPS)

from concourse.mybir import AluOpType as A, ActivationFunctionType as F

N, STEPS, W, R, P = 4, 4, 2048, 4096, 256
PIECES = [(12, 16, "v", 64), (8, 12, "a", 32), (4, 8, "v", 64), (0, 4, "v", 32)]
GROUPS = [(0, 1), (2, 3)]
NPC = len(PIECES)
TW = W + P
HEXP = "vvvgvavgvvvgvavg"

SCRATCH = {
    "HD": ("sbuf", [128, R], "bfloat16"), "OW": ("sbuf", [128, W], "int32"), "MK": ("sbuf", [128, 128], "int32"),
    "MB": ("sbuf", [128, 128], "bfloat16"), "WT": ("sbuf", [128, 1], "bfloat16"), "TI": ("sbuf", [128, 1], "int32"),
    "YO": ("sbuf", [128, W], "float32"), "MZ": ("sbuf", [128, TW], "float32"), "NM": ("sbuf", [128, TW], "float32"),
    "ZP": ("sbuf", [128, W + 8], "float32"), "YM": ("sbuf", [128, W], "float32"),
    "CM": ("sbuf", [128, 2048], "bfloat16"), "SR": ("sbuf", [128, 2048], "bfloat16"),
    "BA": ("sbuf", [2, 128], "bfloat16"), "BR": ("sbuf", [2, 128], "bfloat16"),
    "CA": ("sbuf", [2, 64], "bfloat16"), "CR": ("sbuf", [2, 64], "bfloat16"),
    "HX": ("sbuf", [128, 16 * P], "bfloat16"), "AB": ("sbuf", [128, 16 * P], "bfloat16"),
}
for _d, _w, _ns in (("float32", 1, "SC SQ TH BIG SB KB"), ("int32", 1, "PI SI SJ"),
                    ("bfloat16", 128, "ON B1 BO HB ID IH NI S1 S2 DB BW G0"),
                    ("float32", 16, "IK OH T0 TR XF FR AL AM DW DT XQ DU T2 T3 DM DX"), ("int32", 16, "UI UA UB UP UX OI"),
                    ("uint16", 16, "LX LA SL EL"), ("bfloat16", 512, "WU HL"), ("float32", 512, "DG"),
                    ("float32", 64, "IQ MQ RS ZE UM US ZM ZS EM ES FM FS"), ("float32", 128, "JS G1"),
                    ("float32", P, "ZA ZB DZ NA DE"), ("int32", P, "NX NN FD CL"), ("uint16", P, "LP"),
                    ("bfloat16", P, "NB Y SG E4 DS TD QD")):
    for _n in _ns.split():
        SCRATCH[_n] = ("sbuf", [128, _w], _d)
for _b in range(8):
    SCRATCH["ps%d" % _b] = ("psum", [128, 512], "float32")
for _t in range(STEPS + 1):
    SCRATCH["hb%d" % _t] = ("sbuf", [128, P], "bfloat16")
    SCRATCH["hn%d" % _t] = ("sbuf", [128, P], "bfloat16")
for _p in range(NPC):
    SCRATCH["D%d" % _p] = ("sbuf", [128, 256 * (PIECES[_p][1] - PIECES[_p][0])], "bfloat16")
SEMAPHORES = ["qv", "qa", "qp", "qg", "ls"] + ["dm%d" % k for k in range(24)] + ["ar%d" % t for t in range(1, STEPS + 1)]


def rank_program(g, core, T, topo):
    rank = T.rank_of(core)
    if rank is None:
        return
    dst = T.cores[(rank + 1) % N]
    rid, pid, _e = topo.addr(dst)
    mask = topo.mask(core, dst)
    ne = len(topo.engines(core, dst))
    eng = {"v": g.vector, "a": g.scalar, "p": g.tensor, "g": g, "s": g.sync}
    CY = 1.0e-3
    ops, pr = [], [0.0]

    def r(n, lo=0, hi=None, st=1):
        return (n, lo, SCRATCH[n][1][1] if hi is None else hi, st)

    def ap(x):
        if not isinstance(x, tuple):
            return x
        b, lo, hi, st = x
        if SCRATCH[b][1][0] == 2:
            return T[b][0:2, lo:hi]
        return T[b][:, lo:hi] if st == 1 else T[b][:, lo:hi:st]

    def cnt(x):
        return -(-(x[2] - x[1]) // x[3])

    def ps(x):
        return isinstance(x, tuple) and x[0][:2] == "ps"

    def two(*xs):
        return all(SCRATCH[x[0]][2] in ("bfloat16", "uint16") for x in xs)

    def op(q, fn, rd, wr, dur, sem=None, lat=0.0):
        ops.append({"q": q, "fn": fn, "rd": [x for x in rd if isinstance(x, tuple)], "wr": wr, "dur": dur,
                    "sem": sem, "lat": lat, "pr": pr[0]})

    def tt(o, a, b, f):
        c = cnt(o) * (1 if ps(a) or ps(b) else 2)
        op("v", lambda e: e.tensor_tensor(out=ap(o), in0=ap(a), in1=ap(b), op=f), [a, b], [o], max(64, c) * CY)

    def ts(o, a, s1, f0, s2=None, f1=None):
        c = cnt(o) * (0.5 if two(o, a) else 1)
        if f1 is None:
            fn = lambda e: e.tensor_scalar(out=ap(o), in0=ap(a), scalar1=ap(s1), scalar2=None, op0=f0)
        else:
            fn = lambda e: e.tensor_scalar(out=ap(o), in0=ap(a), scalar1=ap(s1), scalar2=ap(s2), op0=f0, op1=f1)
        op("v", fn, [a, s1, s2], [o], max(64, c) * CY)

    def cp(o, a):
        c = cnt(o) * (0.5 if two(o, a) else 1)
        op("v", lambda e: e.tensor_copy(out=ap(o), in_=ap(a)), [a], [o], max(64, c) * CY)

    def scan(o, a, b, ini=0.0, o0=A.mult, o1=A.add):
        op("v", lambda e: e.tensor_tensor_scan(out=ap(o), data0=ap(a), data1=ap(b), initial=ap(ini), op0=o0, op1=o1),
           [a, b, ini], [o], max(64, cnt(o)) * CY)

    def ms(o, k):
        op("v", lambda e: e.memset(ap(o), k), [], [o], max(64, cnt(o) * (0.5 if two(o) else 1)) * CY)

    def act(o, a, f, bias=0.0, scale=1.0):
        op("a", lambda e: e.activation(out=ap(o), in_=ap(a), func=f, bias=ap(bias), scale=ap(scale)), [a, bias, scale], [o],
           max(64, cnt(o)) * CY + 0.03)

    def gat(q, o, w, off, in1=None):
        d = 0.05 + 1.5 * cnt(o) * CY
        if q == "a":
            op("a", lambda e: e.activation(out=ap(o), in_=ap(w).indirect(ap(off)), func=F.Copy), [w, off], [o], d + 0.015)
        elif in1 is None:
            op("v", lambda e: e.tensor_scalar(out=ap(o), in0=ap(w).indirect(ap(off)), scalar1=-1.0, scalar2=None, op0=A.mult),
               [w, off], [o], d)
        else:
            op("v", lambda e: e.tensor_tensor(out=ap(o), in0=ap(w).indirect(ap(off)), in1=ap(in1), op=A.subtract),
               [w, off, in1], [o], d)

    def mm(o, pairs, x4=1):
        def fn(e):
            last = None
            for k, (l, x) in enumerate(pairs):
                last = e.matmul(ap(o), ap(l), ap(x), k == 0, k == len(pairs) - 1)
            return last
        op("p", fn, [y for x in pairs for y in x], [o], len(pairs) * max(64, cnt(o)) * CY * x4)

    ndma = [0]

    def dma(q, o_fn, i_fn, rd, wr, dur):
        s = "dm%d" % ndma[0]
        ndma[0] += 1
        op(q, lambda e: e.dma_start(out=o_fn(), in_=i_fn()), rd, wr, 0.1, sem=(s, 16), lat=dur)

    dma("s", lambda: T.MK[:], lambda: T.marks[:], [], [r("MK")], 2.0)
    dma("a", lambda: T.hb0[:], lambda: T.h0[:], [], [r("hb0")], 2.0)
    for b in range(4):
        lo, hi = 512 * b, 512 * b + 512
        dma("s", lambda lo=lo, hi=hi: T.OW[:, lo:hi], lambda lo=lo, hi=hi: T.owner[:, lo:hi], [], [r("OW", lo, hi)], 2.5 + b)
    dma("s", lambda: T.WT[:], lambda: T.w[:], [], [r("WT")], 2.0)
    dma("s", lambda: T.HD[:], lambda: T.hdr[:], [], [r("HD")], 7.0)
    dma("s", lambda: T.TI[:], lambda: T.th[:], [], [r("TI")], 3.0)

    def iota(o, pat, base, cm):
        op("g", lambda e: e.iota(ap(o), pat, base, cm, allow_small_or_imprecise_dtypes=True), [], [o],
           0.13 + 2 * cnt(o) * CY)

    def sel(o, a, pat, f, base, cm, fill=0.0):
        op("g", lambda e: e.affine_select(out=ap(o), in_=ap(a), pattern=pat, compare_op=f, fill=fill, base=base,
                                          channel_multiplier=cm), [a], [o], 0.17 + 2 * cnt(o) * CY)
    iota(r("PI"), [[0, 1]], 0, 1)
    ms(r("ON"), 1.0)
    ts(r("SI"), r("PI"), 15, A.bitwise_and)
    cp(r("SC"), r("SI"))
    sel(r("B1"), r("ON"), [[-16, 8], [0, 16]], A.is_ge, 0, 1)
    sel(r("BO"), r("B1"), [[16, 8], [0, 16]], A.is_ge, 15, -1)
    iota(r("IK"), [[1, 16]], 0, 0)
    ts(r("OH"), r("IK"), r("SC"), A.is_equal)
    for k in range(16):
        act(r("SR", 128 * k, 128 * k + 128), r("BO"), F.Copy, 0.0, r("OH", k, k + 1))
    cp(r("MB"), r("MK"))
    ms(r("ZP", 0, 8), 0.0)
    for b in range(4):
        lo, hi = 512 * b, 512 * b + 512
        for k in range(4 * b, 4 * b + 4):
            mm(r("ps%d" % b, 128 * (k % 4), 128 * (k % 4) + 128), [(r("SR", 128 * k, 128 * k + 128), r("MB"))])
        m, n2 = r("ps%d" % b), r("ps%d" % (4 + b))
        act(n2, m, F.Copy, 8192.0, -8192.0)
        act(r("NM", lo, hi), m, F.Copy, -1 / 4096, 8192.0)
        tt(r("MZ", lo, hi), n2, r("OW", lo, hi), A.subtract)
        scan(r("ZP", 8 + lo, 8 + hi), r("NM", lo, hi), r("MZ", lo, hi), r("ZP", 7 + lo, 8 + lo) if b else 0.0, A.add, A.min)
    cp(r("ZP", 7, 8), r("ZP", W + 7, W + 8))
    for n in ("WU", "DG", "HL"):
        ms(r(n), 0.0)
    for k in range(4):
        ms(r("CM", 512 * k, 512 * k + 512), 0.0)
    ts(r("SJ"), r("SI"), 2, A.arith_shift_right)
    cp(r("SQ"), r("SJ"))
    iota(r("IQ"), [[0, 16], [1, 4]], 0, 0)
    ts(r("MQ"), r("IQ"), r("SQ"), A.is_equal)
    ts(r("RS"), r("IQ"), 0.0, A.is_gt)
    ts(r("BW"), r("BO"), r("WT"), A.mult)
    for s in range(4):
        cp(r("WU", 128 * s + s, 128 * s + 128, 4), r("BW", s, 128, 4))
    sel(r("ID"), r("ON"), [[-1, 128]], A.is_equal, 0, 1)
    act(r("NI"), r("ID"), F.Copy, 0.0, -1.0)
    for s in range(16):
        act(r("CM", 128 * s + s, 128 * s + 128, 16), r("BO", 0, 128, 16), F.Copy)
    cp(r("TH"), r("TI"))
    ts(r("BIG"), r("SC"), 4.0, A.mult, 4096.0, A.add)
    ts(r("SB"), r("SC"), -1.0, A.mult, 0.5, A.add)
    for s in range(4):
        act(r("DG", 128 * s + s, 128 * s + 128, 4), r("ID", s, 128, 4), F.Copy)
    sel(r("S1"), r("ON"), [[-1, 128]], A.is_equal, 1, 1)
    sel(r("S2"), r("ON"), [[-1, 128]], A.is_equal, -15, 1)
    tt(r("S1"), r("S1"), r("BO"), A.mult)
    tt(r("S2"), r("S2"), r("BO"), A.mult)
    tt(r("S2"), r("S2"), r("S1"), A.subtract)
    tt(r("DB"), r("S2"), r("ID"), A.add)
    iota(r("JS"), [[0, 8], [1, 16]], 0, 0)
    ts(r("G1"), r("JS"), r("SC"), A.is_ge, 2.0, A.mult)
    ts(r("G0"), r("G1"), -1.0, A.add)
    ts(r("HB"), r("BO"), 0.5, A.mult)
    for s in range(4):
        cp(r("HL", 128 * s + s, 128 * s + 128, 4), r("HB", s, 128, 4))
    iota(r("BA"), [[0, 8], [16, 16]], 0, 0)
    sel(r("BR"), r("BA"), [[0, 128]], A.is_equal, 0, 1, 1.0)
    iota(r("CA"), [[0, 4], [256, 4], [0, 4]], 0, 0)
    sel(r("CR"), r("CA"), [[0, 64]], A.not_equal, 0, 1, 1.0)
    ts(r("IH"), r("ID"), 0.5, A.mult)
    iota(r("T0"), [[16, 16]], W, 0)
    ts(r("TR"), r("T0"), r("SC"), A.add)
    ms(r("ZE"), 8192.0)
    ms(r("KB"), 8192.0)
    for ks in GROUPS:
        c0 = min(PIECES[k][0] for k in ks)
        ms(r("DU", c0, c0 + 1), 0.0)

    SZ = r("ZP", 8, 8 + W)

    def front(t):
        hb, u = "hb%d" % t, r("ps4", 0, 64)
        mm(u, [(r("WU", 128 * s, 128 * s + 128), r(hb, s, P, 4)) for s in range(4)])
        tt(r("UM"), u, r("MQ"), A.mult)
        scan(r("US"), r("RS"), r("UM"))
        cp(r("UI"), r("US", 3, 64, 4))
        ts(r("UA"), r("UI"), 4095, A.bitwise_and)
        ts(r("UB"), r("UA"), 32, A.add)
        tt(r("UP"), r("UA"), r("UB"), A.mult)
        ts(r("UX"), r("UP"), 5, A.arith_shift_right, 2032, A.bitwise_and)
        ts(r("LX"), r("UX"), r("SC"), A.add)
        ts(r("XF"), r("UX"), r("SC"), A.add)
        for s in range(16):
            o, i = r("HX", s, 16 * P, 16), r(hb)
            if HEXP[s] == "a":
                act(o, i, F.Copy)
            elif HEXP[s] == "v":
                cp(o, i)
            else:
                sel(o, i, [[0, P]], A.is_gt, 1, 0)
        gat("v", r("LP"), SZ, r("LX"))

    def before(t):
        zw, za = r("ps4", 64, 128), r("ps4", 128, 384)
        gat("a", r("ZA"), SZ, r("LX"))
        mm(zw, [(r("DG", 128 * s, 128 * s + 128), r("ZA", s, P, 4)) for s in range(4)], x4=4)
        tt(r("ZM"), zw, r("MQ"), A.mult)
        scan(r("ZS"), r("RS"), r("ZM"))
        cp(r("OI"), r("ZS", 3, 64, 4))
        tt(r("FR"), r("ZS", 3, 64, 4), r("OI"), A.subtract)
        ts(r("AL"), r("FR"), 4096.0, A.mult, 7.0, A.add)
        tt(r("AM"), r("AL"), r("XF"), A.add)
        cp(r("LA"), r("AM"))
        gat("a", r("ZB"), r("ZP"), r("LA"))
        act(za, r("ZA"), F.Copy)
        tt(r("DZ"), r("ZB"), za, A.subtract)

    def wrap(c0, c1):
        return [(r("BR"), r("CR", 0, 4 * (c1 - c0)))] + \
            [(r("HL", 128 * s, 128 * s + 128), r("Y", 16 * c0 + s, 16 * c1, 4)) for s in range(4)]

    def rules(t, p):
        c0, c1, q, ck = PIECES[p]
        nl, q4, L0, L1 = 16 * (c1 - c0), 4 * (c1 - c0), 16 * c0, 16 * c1
        hb, D, bk = "hb%d" % t, "D%d" % p, "ps%d" % p
        for l in range(0, nl, ck):
            v = r(D, 16 * l, 16 * (l + ck))
            lp, hx, ab = r("LP", L0 + l, L0 + l + ck), r("HX", 16 * (L0 + l), 16 * (L0 + l + ck)), \
                r("AB", 16 * (L0 + l), 16 * (L0 + l + ck))
            if q == "v":
                gat("v", v, r("HD"), lp, hx)
                act(ab, v, F.Abs)
            else:
                df = r("ps%d" % (6 + (l // ck) % 2), 0, 16 * ck)
                gat("a", v, r("HD"), lp)
                mm(df, [(r("NI"), hx), (r("ID"), v)])
                act(ab, df, F.Abs)
        d, w0, ad, dl, eb, dn = [r(bk, 64 * k, 64 * k + nl) for k in range(6)]
        ew = r(bk, 448, 448 + q4)
        x = lambda n: r(n, L0, L1)
        y = lambda n, st=1: r(n, 4 * c0 + st - 1, 4 * c1, st)
        mm(d, [(r("CM", 128 * s, 128 * s + 128), r("AB", 16 * L0 + s, 16 * L1, 16)) for s in range(16)])
        ts(x("NA"), d, r("TH"), A.is_lt, r("BIG"), A.mult)
        tt(x("NX"), x("NA"), d, A.max)
        ts(x("NN"), x("NX"), 2, A.arith_shift_right, 15, A.bitwise_and)
        cp(x("NB"), x("NN"))
        mm(dl, [(r("DB"), x("NB"))])
        for k in range(5):
            if k:
                act(x("SG"), eb, F.Sign, r("SB"))
            if k == 4:
                act(x("E4"), eb, F.Copy)
            tt(x("Y"), x("SG") if k else r("G0", 0, nl), dl, A.mult)
            mm(eb, [(r("HB"), x("Y"))])
            if k == 3:
                mm(ew, wrap(c0, c1))
                tt(y("EM"), ew, y("MQ"), A.mult)
                scan(y("ES"), y("RS"), y("EM"))
                cp(r("EL", c0, c1), y("ES", 4))
        gat("a", x("DS"), r(D), r("EL", c0, c1))
        if q == "a":
            mm(ad, [(r("ID"), x("DS")), (r("NI"), x(hb))])
        act(ad, ad if q == "a" else x("DS"), F.Abs)
        mm(w0, [(r("IH"), x("DS")), (r("IH") if q == "a" else r("ID"), x(hb))])
        ts(x("FD"), w0, -0.25, A.add)
        tt(x("TD"), x("FD"), ad, A.subtract)
        tt(dn, x("E4"), eb, A.is_equal)
        tt(x("QD"), x("TD"), dn, A.mult)
        tt(x("hn%d" % t), x("QD"), ad, A.add)

    def send(t):
        nh, hn, arr = "hb%d" % (t + 1), r("hn%d" % t), "ar%d" % (t + 1)
        op("g", lambda e: e.remote_dma(T[nh][:], ap(hn), T.sem[arr], T.sem.ls, pid, rid, mask),
           [hn], [r(nh)], 1.5, sem=(arr, ne), lat=2.0)

    def calls(t, ks):
        c0, c1 = min(PIECES[k][0] for k in ks), max(PIECES[k][1] for k in ks)
        L0, L1 = 16 * c0, 16 * c1
        e4p, za = r("ps4", 384, 384 + L1 - L0), r("ps4", 128 + L0, 128 + L1)
        y = lambda n, st=1: r(n, 4 * c0 + st - 1, 4 * c1, st)
        x = lambda n, a=0, b=0: r(n, c0 + a, c1 - b)
        z = lambda n: r(n, L0, L1)
        fw = r("ps5", 4 * c0, 4 * c1)
        mm(fw, wrap(c0, c1))
        tt(y("FM"), fw, y("MQ"), A.mult)
        scan(y("FS"), y("RS"), y("FM"))
        tt(x("DW"), y("FS", 4), y("ES", 4), A.is_equal)
        tt(x("DT"), x("DW"), x("TR"), A.mult)
        tt(x("XQ"), x("DT"), x("XF"), A.max)
        tt(x("DU", 1), x("XQ", 1), x("XQ", 0, 1), A.is_equal)
        tt(x("T2", 2), x("XQ", 2), x("XQ", 0, 2), A.is_equal)
        tt(x("T3", 3), x("XQ", 3), x("XQ", 0, 3), A.is_equal)
        tt(x("DU", 2), x("DU", 2), x("T2", 2), A.max)
        tt(x("DU", 3), x("DU", 3), x("T3", 3), A.max)
        tt(x("DM"), x("DU"), x("TR"), A.mult)
        tt(x("DX"), x("DM"), x("XQ"), A.max)
        cp(x("SL"), x("DX"))
        ts(e4p, z("E4"), r("SC"), A.is_equal)
        tt(z("DE"), z("DZ"), e4p, A.mult)
        tt(z("CL"), z("DE"), za, A.add)
        for c in range(c1 - 4, c0 - 1, -4):
            off, col = r("SL", c, c + 4), r("CL", 16 * c, 16 * c + 64)
            op("v", lambda e, off=off, col=col: e.tensor_copy(out=ap(r("MZ")).indirect(ap(off)), in_=ap(col)),
               [off, col], [r("MZ")], 0.05 + 64 * 3.0 * CY)
            op("a", lambda e, off=off: e.activation(out=ap(r("NM")).indirect(ap(off)), in_=ap(r("ZE")), func=F.Silu),
               [off, r("ZE")], [r("NM")], 0.065 + 64 * 3.0 * CY)

    for t in range(STEPS):
        front(t)
        for p in range(NPC):
            pr[0] = 1.0 * (NPC - 1 - p)
            rules(t, p)
        send(t)
        pr[0] = 0.0
        before(t)
        for ks in GROUPS:
            calls(t, ks)
        if t < STEPS - 1:
            scan(SZ, r("NM", 0, W), r("MZ", 0, W), 0.0, A.add, A.min)
            cp(r("ZP", 7, 8), r("ZP", W + 7, W + 8))
    for b in range(4):
        lo, hi, m = 512 * b, 512 * b + 512, r("ps%d" % b)
        act(m, r("NM", lo, hi), F.Relu, r("KB"), -2.0)
        tt(r("YO", lo, hi), m, r("MZ", lo, hi), A.subtract)
        dma("s", lambda lo=lo, hi=hi: T.yo[:, lo:hi], lambda lo=lo, hi=hi: T.YO[:, lo:hi], [r("YO", lo, hi)], [], 5.0)
        act(r("YM", lo, hi), m, F.Copy, 1.0, -1 / 8192)
    dma("s", lambda: T.ym[:], lambda: T.YM[0:128:16, :], [r("YM")], [], 2.0)
    dma("s", lambda: T.yh[:], lambda: T["hb%d" % STEPS][:], [r("hb%d" % STEPS)], [], 2.0)

    emit(g, T, ops, eng, ne)


def meet(x, y):
    if x[1] >= y[2] or y[1] >= x[2]:
        return False
    return not (x[3] == y[3] and x[3] > 1 and (x[1] - y[1]) % x[3])


def covers(x, y):
    return x[3] == 1 and x[1] <= y[1] and x[2] >= y[2]


def emit(g, T, ops, eng, ne):
    n = len(ops)
    dep = [dict() for _ in range(n)]
    hist = {}
    for i, o in enumerate(ops):
        for wr, xs in ((False, o["rd"]), (True, o["wr"])):
            for x in xs:
                psum = x[0][:2] == "ps"
                for (j, y, w) in hist.get(x[0], []):
                    same = ops[j]["q"] == o["q"] and ops[j]["sem"] is None
                    if (wr or w) and meet(x, y):
                        wait = (w or not same) and not (same and o["q"] == "p" and w and wr)
                        dep[i][j] = dep[i].get(j, False) or wait
                    elif psum:
                        dep[i][j] = dep[i].get(j, False) or not same
        for wr, xs in ((False, o["rd"]), (True, o["wr"])):
            for x in xs:
                h = hist.setdefault(x[0], [])
                if wr:
                    h[:] = [z for z in h if z[0] == i or not covers(x, z[1])]
                h.append((i, x, wr))
    succ = [[] for _ in range(n)]
    for i in range(n):
        for j in dep[i]:
            succ[j].append(i)
    HOP = 0.1
    tail = [0.0] * n
    for i in range(n - 1, -1, -1):
        o = ops[i]
        tail[i] = o["dur"] + o["lat"] + max([tail[k] + HOP for k in succ[i]], default=0.0)
    left = [len(dep[i]) for i in range(n)]
    avail = [0.0] * n
    ready = {q: [] for q in eng}
    for i in range(n):
        if not left[i]:
            ready[ops[i]["q"]].append(i)
    free = {q: 0.0 for q in eng}
    order = []
    while len(order) < n:
        t0, q = min((max(free[q], min(avail[i] for i in ready[q])), q) for q in eng if ready[q])
        i = max((k for k in ready[q] if avail[k] <= t0 + 1e-9), key=lambda k: (tail[k] + ops[k]["pr"], -k))
        ready[q].remove(i)
        o = ops[i]
        free[q] = t0 + o["dur"]
        for k in succ[i]:
            avail[k] = max(avail[k], t0 + o["dur"] + o["lat"] + HOP if dep[k][i] else t0)
            left[k] -= 1
            if not left[k]:
                ready[ops[k]["q"]].append(k)
        order.append(i)
    count = {q: 0 for q in eng}
    mark, know, after, place = {}, {q: {} for q in eng}, {}, {}
    final = {}
    for i in order:
        o = ops[i]
        q = o["q"]
        kn = know[q]
        for j in sorted((j for j in dep[i] if dep[i][j]), key=lambda j: -place[j]):
            s, v = mark[j]
            if kn.get(s, 0) >= v:
                continue
            eng[q].wait_ge(T.sem[s], v)
            for s2, v2 in after[j].items():
                if kn.get(s2, 0) < v2:
                    kn[s2] = v2
        ins = o["fn"](eng[q])
        remote = o["sem"] is not None and o["sem"][0][:2] == "ar"
        if o["sem"] is None:
            count[q] += 1
            mark[i] = ("q" + q, count[q])
            ins.then_inc(T.sem["q" + q], 1)
        else:
            mark[i] = o["sem"]
            if not remote:
                ins.then_inc(T.sem[o["sem"][0]], 16)
        final[mark[i][0]] = mark[i][1]
        after[i] = {} if remote else dict(kn)
        after[i][mark[i][0]] = mark[i][1]
        place[i] = len(place)
    for s, v in final.items():
        g.wait_ge(T.sem[s], v)
    g.wait_ge(T.sem.ls, ne * STEPS)
